import numpy as np, ml_dtypes
CORES = [35,38,43,46]
N = 4
BF = ml_dtypes.bfloat16
def f(rng, *shape):
    return (rng.standard_normal(shape, dtype=np.float32) * np.exp2(rng.integers(-2, 3, shape[:-1] + (1,)))).astype(BF)
def wide(rng, *shape):
    v = f(rng, *shape).astype(np.float32); k = shape[:-2] + (1, shape[-1])
    return (v * np.exp2(rng.integers(-6, 7, k)) * (rng.random(k) > 0.0625)).astype(BF)
def gentries(a):
    return np.ascontiguousarray(a.reshape(8, 16, -1).transpose(0, 2, 1)).reshape(8, -1)
def gtable(e):
    e = np.asarray(e); return np.ascontiguousarray(e.reshape(8, -1, 16).transpose(0, 2, 1)).reshape(128, -1).astype(np.int32)
L, K, R, D = 4096, 512, 4, 2048
def corner(rng):
    return rng.integers(0, 4096 - D, (2, 1, 8, 1))
def walk(rng):
    v = np.repeat(rng.integers(-3, 4, (N, 8, L // 64)), 64, axis=2) + rng.integers(-1, 2, (N, 8, L))
    m = (rng.integers(0, D + 1, (N, 8, 1)) + np.add.accumulate(v, axis=2)) % (2 * D)
    return D - np.abs(m - D)
def listeners(rng, o):
    return rng.integers(D, L - 1, (N, 8, K)), o[0] + rng.integers(0, D + 1, (N, 8, K)), o[1] + rng.integers(0, D + 1, (N, 8, K))
def packed(X, Y, s, t, x, z):
    return {"track": (X * 4096 + Y).astype(np.int32), "sound": s, "when": np.stack([gtable(a) for a in t]), "place": np.stack([gtable(a) for a in x * 4096 + z])}
def setup_inputs(rng):
    o = corner(rng); t, x, z = listeners(rng, o)
    return packed(o[0] + walk(rng), o[1] + walk(rng), f(rng, N, 128, L), t, x, z)
def setup_inputs_ends(rng):
    o = np.zeros((2, 1, 8, 1), np.int64); o[:, :, 1::2] = 4095 - D
    X, Y = o[0] + walk(rng), o[1] + walk(rng); t, x, z = listeners(rng, o)
    for g in range(8):
        q = int(rng.integers(0, N)); c = int(o[0, 0, g, 0]); near, far = (c, c + D) if g % 2 == 0 else (c + D, c)
        X[q, g, :D + 1] = near; Y[q, g, :D + 1] = near
        t[:, g, 0] = D; x[:, g, 0] = far; z[:, g, 0] = far
        for r in range(N):
            p = (r + 1) % N; t[r, g, K - 1] = L - 2; x[r, g, K - 1] = X[p, g, L - 2]; z[r, g, K - 1] = Y[p, g, L - 2]
    return packed(X, Y, f(rng, N, 128, L), t, x, z)
def setup_inputs_jumps(rng):
    o = corner(rng); t, x, z = listeners(rng, o)
    return packed(o[0] + rng.integers(0, D + 1, (N, 8, L)), o[1] + rng.integers(0, D + 1, (N, 8, L)), f(rng, N, 128, L), t, x, z)
def setup_inputs_still(rng):
    o = corner(rng); t, x, z = listeners(rng, o); X, Y = o[0] + walk(rng), o[1] + walk(rng)
    q = int(rng.integers(0, N)); r = (q + 1) % N; w = (q + 2) % N
    X[q] = X[q, :, :1].copy(); Y[q] = Y[q, :, :1].copy()
    for a in (t, x, z): a[r, :4] = a[r, :4, :1].copy()
    t[w] = np.sort(t[w], axis=1); x[w] = x[w, :, :1].copy(); z[w] = z[w, :, :1].copy()
    return packed(X, Y, f(rng, N, 128, L), t, x, z)
def setup_inputs_sizes(rng):
    d = np.array([0, 4094, 3, 4000, 64, 3000, 500, 2049]).reshape(1, 8, 1)
    o = rng.integers(0, 4096 - d, (2, 1, 8, 1))
    h = lambda n: rng.integers(0, d + 1, (N, 8, n))
    t = rng.integers(d, L - 1, (N, 8, K)); t[:, 0, 0] = 0
    return packed(o[0] + h(L), o[1] + h(L), f(rng, N, 128, L), t, o[0] + h(K), o[1] + h(K))
def setup_inputs_spread(rng):
    d = setup_inputs(rng); d["sound"] = wide(rng, N, 128, L); return d
def check_inputs(d):
    bad = []; tr = np.asarray(d["track"]).astype(np.int64); pl = np.asarray(d["place"]).astype(np.int64); wh = np.asarray(d["when"]).astype(np.int64)
    if not np.isfinite(np.asarray(d["sound"]).astype(np.float32)).all(): bad.append("finite")
    if tr.min() < 0 or tr.max() >= 4096 * 4096: bad.append("track")
    if pl.min() < 0 or pl.max() >= 4096 * 4096: bad.append("place")
    if wh.min() < 0 or wh.max() > L - 2: bad.append("when")
    ok = True
    for r in range(N):
        t = gentries(wh[r]); w = gentries(pl[r])
        for q in range(N):
            e = np.clip(t, 0, L - 2)
            for i in range(R):
                v = np.take_along_axis(tr[q], e, 1)
                e = t - np.maximum(np.abs((v >> 12) - (w >> 12)), np.abs((v & 4095) - (w & 4095)))
                ok = ok and bool(e.min() >= 0) and bool(e.max() <= L - 2); e = np.clip(e, 0, L - 2)
    if not ok: bad.append("inside")
    return bad
def reference(track, sound, when, place):
    y = np.zeros((N, 128, K), np.float32); s = sound.astype(np.float32).reshape(N, 8, 16, L); tr = track.astype(np.int64)
    for r in range(N):
        t = gentries(when[r]).astype(np.int64); w = gentries(place[r]).astype(np.int64)
        for q in range(N):
            e = t
            for i in range(R):
                v = np.take_along_axis(tr[q], e, 1)
                e = t - np.maximum(np.abs((v >> 12) - (w >> 12)), np.abs((v & 4095) - (w & 4095)))
            u = np.take_along_axis(s[q], e[:, None, :], 2) + np.take_along_axis(s[q], e[:, None, :] + 1, 2)
            y[r] += u.astype(BF).astype(np.float32).reshape(128, K)
    return {"y": y}

@@ -1,0 +1,326 @@
+from concourse.bass import DstId, RemoteDMATransfer
+from concourse.mybir import AluOpType as Op, ActivationFunctionType as Act
+
+N, L, K = 4, 4096, 512
+HALF = 2048.0
+BIG = 32768.0
+
+SCRATCH = {
+    "Si": ("sbuf", [128, 96], "int32"), "Pl": ("sbuf", [128, 32], "int32"), "tz": ("sbuf", [128, 32], "int32"),
+    "Sh": ("sbuf", [128, 96], "float16"),
+    "offq": ("sbuf", [128, N * 32], "uint16"),
+    "WA": ("sbuf", [128, N * 128], "float16"), "WZ": ("sbuf", [128, N * 128], "float16"),
+    "tr0": ("sbuf", [128, 256], "int32"), "tr1": ("sbuf", [128, 256], "int32"),
+    "xi0": ("sbuf", [128, 256], "int32"), "xi1": ("sbuf", [128, 256], "int32"),
+    "xh0": ("sbuf", [128, 256], "float16"), "xh1": ("sbuf", [128, 256], "float16"),
+    "win": ("sbuf", [128, L], "float32"), "U": ("sbuf", [128, L], "bfloat16"),
+    "uo": ("sbuf", [128, N * K], "bfloat16"), "ui": ("sbuf", [128, N * K], "bfloat16"),
+    "ysb": ("sbuf", [128, K], "float32"),
+    "V": ("sbuf", [128, 352], "int32"), "Vm": ("sbuf", [128, 64], "int32"), "J": ("sbuf", [128, 64], "float32"),
+    "Ip": ("sbuf", [128, 384], "float16"), "Irep": ("sbuf", [128, 1024], "bfloat16"),
+    "R": ("sbuf", [128, 320], "float16"), "RC": ("sbuf", [128, 256], "float16"),
+    "wk": ("sbuf", [128, 4], "float32"), "pat": ("sbuf", [128, 128], "float32"),
+}
+for _c in range(N):
+    SCRATCH["gb%d" % _c] = ("sbuf", [128, K], "float16")
+    SCRATCH["sc%d" % _c] = ("sbuf", [128, 128], "float32")
+    SCRATCH["tt%d" % _c] = ("sbuf", [128, 32], "float32")
+    SCRATCH["off%d" % _c] = ("sbuf", [128, 32], "uint16")
+for _b in range(8):
+    SCRATCH["pb%d" % _b] = ("psum", [128, 512], "float32")
+
+SEMAPHORES = (["sV", "sA", "sP", "sG", "lw", "lp", "lt0", "lt1", "ls0", "ls1", "acc", "left", "st0", "st1"]
+              + ["%s%d" % (n, q) for n in ("qo", "qa", "qz", "qu") for q in range(N)])
+
+ORDER_A = [('G', 3, 1, 192, 320), ('G', 0, 1, 128, 384), ('G', 1, 1, 0, 512), ('G', 0, 2, 0, 256), ('G', 2, 2, 0, 384), ('G', 1, 2, 0, 384), ('G', 0, 3, 0, 320), ('G', 2, 3, 0, 512), ('G', 1, 3, 256, 256), ('G', 0, 4, 0, 192), ('G', 3, 2, 0, 384), ('G', 1, 4, 0, 448), ('G', 0, 5, 256, 256), ('G', 2, 4, 0, 512), ('G', 3, 3, 320, 192), ('G', 1, 5, 0, 512), ('G', 2, 5, 256, 256), ('G', 3, 4, 0, 256), ('G', 3, 5, 0, 256)]
+ORDER_V = [('G', 2, 1, 0, 512), ('G', 0, 1, 0, 128), ('G', 3, 1, 0, 192), ('S', 2, 1), ('S', 0, 1), ('C', 0, 1), ('C', 2, 1), ('G', 0, 2, 256, 256), ('S', 1, 1), ('G', 2, 2, 384, 128), ('C', 1, 1), ('S', 0, 2), ('S', 3, 1), ('C', 0, 2), ('G', 1, 2, 384, 128), ('S', 2, 2), ('G', 0, 3, 320, 192), ('C', 2, 2), ('C', 3, 1), ('S', 1, 2), ('S', 0, 3), ('C', 1, 2), ('C', 0, 3), ('G', 1, 3, 0, 256), ('G', 0, 4, 192, 320), ('S', 1, 3), ('G', 3, 2, 384, 128), ('C', 1, 3), ('S', 0, 4), ('S', 2, 3), ('T', 0, 4), ('G', 1, 4, 448, 64), ('C', 0, 4), ('C', 2, 3), ('G', 0, 5, 0, 256), ('S', 1, 4), ('S', 3, 2), ('T', 1, 4), ('C', 3, 2), ('C', 1, 4), ('G', 3, 3, 0, 320), ('S', 2, 4), ('T', 2, 4), ('C', 2, 4), ('S', 3, 3), ('G', 2, 5, 0, 256), ('C', 3, 3), ('G', 3, 4, 256, 256), ('S', 3, 4), ('T', 3, 4), ('C', 3, 4), ('G', 3, 5, 256, 256)]
+ORDER_P = [(2, 1), (0, 1), (3, 1), (1, 1), (0, 2), (2, 2), (1, 2), (0, 3), (2, 3), (1, 3), (0, 4), (3, 2), (1, 4), (2, 4), (3, 3), (3, 4)]
+
+
+def peers_of(cores, me, topo):
+    c = cores[me]
+    others = [r for r in range(len(cores)) if r != me]
+    return sorted(others, key=lambda r: (topo.chip(cores[r]) == topo.chip(c), topo.die(cores[r]) == topo.die(c), r))
+
+
+def engine_sets(cores, me, topo):
+    c = cores[me]
+    far = [r for r in peers_of(cores, me, topo) if topo.chip(cores[r]) != topo.chip(c)]
+    out, used = {}, set()
+    for n, r in enumerate(far):
+        e = topo.engines(c, cores[r])
+        part = len(e) // len(far)
+        out[r] = (e[n * part:(n + 1) * part], e)
+        used |= set(e)
+    for r in peers_of(cores, me, topo):
+        if r not in far:
+            e = [x for x in topo.engines(c, cores[r]) if x not in used]
+            out[r] = (e, e)
+    return out
+
+
+def bits(e):
+    return sum(1 << x for x in e)
+
+
+def rank_program(g, core, T, topo):
+    me = T.rank_of(core)
+    if me is None:
+        return
+    cores = list(T.cores)
+    S = T.sem
+    peers = peers_of(cores, me, topo)
+    chunk_rank = peers + [me]
+    eng = engine_sets(cores, me, topo)
+    came = {q: engine_sets(cores, q, topo)[me] for q in peers}
+
+    Q = {"V": g.vector, "A": g.scalar, "P": g.tensor, "G": g, "Y": g.sync}
+    count = {"V": 0, "A": 0, "P": 0, "G": 0}
+    seen = {}
+
+    def done(q, ins):
+        count[q] += 1
+        ins.then_inc(S["s" + q], 1)
+        return ("s" + q, count[q])
+
+    def wait(q, *toks):
+        for name, val in toks:
+            if seen.get((q, name), 0) < val:
+                Q[q].wait_ge(S[name], val)
+                seen[(q, name)] = val
+
+    V, A, P, Y = g.vector, g.scalar, g.tensor, g.sync
+    pb = [T["pb%d" % b] for b in range(8)]
+    mine = slice(128 * me, 128 * me + 128)
+
+    Y.dma_start(T.Si[:, 0:32], T.when[:]).then_inc(S.lw, 16)
+    A.dma_start(T.Pl[:], T.place[:]).then_inc(S.lp, 16)
+    for h in range(2):
+        for xy in range(2):
+            (Y, A)[xy].dma_start(T["tr%d" % h][64 * xy:64 * xy + 64, :],
+                                 T.track[:, 2048 * h:2048 * h + 2048]).then_inc(S["lt%d" % h], 16)
+    Y.dma_start(T.U[:, 0:2048], T.sound[:, 0:2048]).then_inc(S.ls0, 16)
+
+    gI = done("G", g.iota(T.V[:, 0:128], [[1, 128]], 0, -1))
+    done("G", g.iota(T.V[:, 288:320], [[1, 4], [4, 4], [16, 2]], 128, -1))
+    gC = done("G", g.iota(T.V[:, 320:352], [[1, 32]], 128, -1))
+    done("G", g.iota(T.V[:, 128:256], [[1, 8], [16, 8], [8, 2]], 0, -1))
+    done("G", g.iota(T.V[:, 256:272], [[34, 4], [16, 2], [8, 2]], 0, -1))
+    gR = done("G", g.iota(T.V[:, 272:288], [[34, 4], [16, 2], [8, 2]], 1, -1))
+
+    vpz = done("V", V.memset(T.pat[:], 0.0))
+    done("V", V.memset(T.Ip[:, 0:128], 0.0))
+    done("V", V.memset(T.Ip[:, 256:384], 0.0))
+    wait("V", gI)
+    vI0 = done("V", V.tensor_scalar(T.Irep[:, 0:128], T.V[:, 0:128], 0.0, None, Op.is_equal))
+    vIp = done("V", V.tensor_scalar(T.Ip[:, 128:256], T.V[:, 0:128], 0.0, None, Op.is_equal))
+    done("V", V.memset(T.wk[0:32, :], 1.0))
+    done("V", V.memset(T.wk[32:64, 0:1], 1.0))
+    done("V", V.memset(T.wk[32:64, 1:2], -1.0))
+    done("V", V.memset(T.wk[32:64, 2:4], 0.0))
+    wait("V", gC)
+    vm = done("V", V.tensor_scalar(T.Vm[0:96, :], T.V[0:96, 288:352], 31, None, Op.bitwise_and))
+    done("V", V.memset(T.wk[64:96, 0:2], 0.0))
+    done("V", V.memset(T.wk[64:96, 2:3], 1.0))
+    done("V", V.memset(T.wk[64:96, 3:4], -1.0))
+    wait("V", vpz, vm)
+    vpat = done("V", V.memset(T.pat[:, 0::4], BIG))
+    vJ = done("V", V.tensor_scalar(T.J[0:96, :], T.Vm[0:96, :], 0.0, None, Op.is_equal))
+    wait("V", gR)
+    vR = done("V", V.tensor_scalar(T.R[:, 1::2], T.V[:, 128:288], 0.0, None, Op.is_equal))
+
+    wait("A", vI0)
+    a = done("A", A.activation(T.Irep[:, 128:256], T.Irep[:, 0:128], Act.Copy))
+    done("A", A.activation(T.WA[96:128, mine], T.Irep[96:128, 0:128], Act.Copy))
+    wait("A", a)
+    a = done("A", A.activation(T.Irep[:, 256:512], T.Irep[:, 0:256], Act.Copy))
+    aW = done("A", A.activation(T.WZ[96:128, mine], T.Irep[96:128, 0:128], Act.Copy))
+    wait("A", a)
+    aI = done("A", A.activation(T.Irep[:, 512:1024], T.Irep[:, 0:512], Act.Copy))
+    wait("A", vJ)
+    for k in range(4):
+        done("A", A.activation(T.RC[0:96, k::4], T.J[0:96, :], Act.Identity, scale=T.wk[0:96, k:k + 1]))
+    wait("A", vR)
+    aR = done("A", A.activation(T.R[:, 0::2], T.R[:, 1::2], Act.Identity, scale=-1.0))
+
+    wait("V", ("lw", 16))
+    v1 = done("V", V.transpose(T.tz[:], T.Si[:, 0:32]))
+    wait("V", ("lp", 16))
+    done("V", V.tensor_scalar(T.Si[:, 32:64], T.Pl[:], 12, None, Op.logical_shift_right))
+    v2 = done("V", V.tensor_scalar(T.Si[:, 64:96], T.Pl[:], 4095, None, Op.bitwise_and))
+    wait("V", v1)
+    vOff = done("V", V.tensor_copy(T.offq[:, 32 * me:32 * me + 32], T.tz[:]))
+    wait("V", v2)
+    vSh = done("V", V.tensor_scalar(T.Sh[:], T.Si[:], -HALF, None, Op.add))
+
+    ax = {}
+    for h in range(2):
+        tr, xi, xh = T["tr%d" % h], T["xi%d" % h], T["xh%d" % h]
+        wait("V", ("lt%d" % h, 32))
+        done("V", V.tensor_scalar(xi[0:64, :], tr[0:64, :], 12, None, Op.logical_shift_right))
+        a = done("V", V.tensor_scalar(xi[64:128, :], tr[64:128, :], 4095, None, Op.bitwise_and))
+        wait("A", a)
+        ax[h] = done("A", A.activation(xh[:], xi[:], Act.Identity, bias=-HALF))
+
+    wait("P", vIp, vSh)
+    for q in range(3):
+        for il in range(8):
+            o = pb[7][32 * q:32 * q + 32, 16 * il:16 * il + 16]
+            P.matmul(o, T.Ip[:, 128 + il:384:8], T.Sh[:, 32 * q:32 * q + 16], True, False)
+            ins = P.matmul(o, T.Ip[:, il:256:8], T.Sh[:, 32 * q + 16:32 * q + 32], False, True)
+    pWA = done("P", ins)
+    for q in range(3):
+        for z in range(4):
+            ins = P.matmul(pb[6][32 * q:32 * q + 32, 32 * z:32 * z + 32], T.Ip[:, 128 + 32 * z:160 + 32 * z],
+                           T.Sh[:, 32 * q:32 * q + 32], True, True)
+    pWZ = done("P", ins)
+    wait("V", pWA)
+    vWA = done("V", V.tensor_copy(T.WA[0:96, mine], pb[7][0:96, 0:128]))
+    wait("V", pWZ)
+    vWZ = done("V", V.tensor_copy(T.WZ[0:96, mine], pb[6][0:96, 0:128]))
+
+    bank = {}
+    for h in range(2):
+        wait("P", ax[h], aI)
+        for k in range(8):
+            b = 4 * h + k // 2
+            if b >= 6:
+                wait("P", vWZ)
+            ins = P.matmul(pb[b][:, 256 * (k % 2):256 * (k % 2) + 256], T.Irep[:, k::8], T["xh%d" % h][:], True, True)
+            if k % 2:
+                bank[b] = done("P", ins)
+    for b in (1, 3, 5, 7):
+        wait("A", bank[b])
+        winA = done("A", A.activation(T.win[:, 512 * b:512 * b + 512], pb[b][:], Act.Copy))
+    for b in (0, 2, 4, 6):
+        wait("V", bank[b])
+        winV = done("V", V.tensor_copy(T.win[:, 512 * b:512 * b + 512], pb[b][:]))
+        if b == 0:
+            wait("Y", winV)
+            Y.dma_start(T.U[:, 2048:4096], T.sound[:, 2048:4096]).then_inc(S.ls1, 16)
+
+    left = [0]
+
+    def to_all(name, width, sem):
+        tr = []
+        for r in peers:
+            rid, pid, _ = topo.addr(cores[r])
+            ap = T[name][:, width * me:width * me + width]
+            tr.append(RemoteDMATransfer(dst_ids=[DstId(rid=rid, pnc=pid)], dma_engine_mask=bits(eng[r][0]),
+                                        remote_sem=S["%s%d" % (sem, me)], src=ap, dst=ap))
+            left[0] += len(eng[r][0])
+        g.remote_dma_fused(tr, local_sem=S.left)
+
+    wait("G", vOff)
+    to_all("offq", 32, "qo")
+    wait("G", aW, vWA)
+    to_all("WA", 128, "qa")
+    wait("G", vWZ)
+    to_all("WZ", 128, "qz")
+    wait("G", ("ls0", 16))
+    g.dma_start(T.U[:, 0:2048], T.sound[:, 1:2049], accum_op=Op.add, max_dma_last_dim=4096).then_inc(S.acc, 16)
+    wait("G", ("ls1", 16))
+    g.dma_start(T.U[:, 2048:4095], T.sound[:, 2049:4096], accum_op=Op.add, max_dma_last_dim=4096).then_inc(S.acc, 16)
+
+    tok = {}
+    allG = [o for o in ORDER_A + ORDER_V if o[0] == "G"]
+
+    def ready(op):
+        kind, c, k = op[:3]
+        if kind == "G":
+            return [("C", c, k - 1)] if k > 1 else []
+        if kind == "P":
+            return [o for o in allG if o[1] == c and o[2] == k]
+        if kind == "S":
+            return [("P", c, k)]
+        if kind == "T":
+            return [("S", c, k)]
+        return [("T" if k == 4 else "S", c, k)]
+
+    def emit(q, op):
+        kind, c, k = op[:3]
+        r = chunk_rank[c]
+        gb, sc, tt, off, ps = T["gb%d" % c], T["sc%d" % c], T["tt%d" % c], T["off%d" % c], pb[c]
+        deps = [tok[d] for d in ready(op)]
+        if kind == "G":
+            c0, n = op[3:]
+            if k == 1:
+                wait(q, winA, winV, vOff if r == me else ("qo%d" % r, len(came[r][0])))
+                lst = T.offq[:, 32 * r + c0 // 16:32 * r + (c0 + n) // 16]
+            else:
+                lst = off[:, c0 // 16:(c0 + n) // 16]
+            wait(q, *deps)
+            if k == 5:
+                wait(q, ("acc", 32))
+                src = T.U[:, :].indirect(lst)
+                dst = (T.ui if r == me else T.uo)[:, K * r + c0:K * r + c0 + n]
+            else:
+                src = T.win[:, :].indirect(lst)
+                dst = gb[:, c0:c0 + n]
+            ins = V.tensor_copy(dst, src) if q == "V" else A.activation(dst, src, Act.Copy)
+        elif kind == "P":
+            if k == 1:
+                wait(q, winA, winV, aR, vWA if r == me else ("qa%d" % r, len(came[r][0])))
+            else:
+                wait(q, tok[("S", c, k - 1)], vWZ if r == me else ("qz%d" % r, len(came[r][0])))
+            tab, lay = (T.WA, 0) if k % 2 else (T.WZ, 128)
+            P.matmul(ps[:, 0:128], tab[0:96, 128 * r:128 * r + 128], T.RC[0:96, lay:lay + 128], True, False)
+            if k % 2:
+                sets = [(128 * s, 128, ps[:, 32 * s:32 * s + 32], 256 + 32 * (s // 2), s == 3) for s in range(4)]
+            else:
+                sets = [(128 * s + 32 * z, 32, ps[32 * z:32 * z + 32, 32 * s:32 * s + 32], 32 * (2 * z + s // 2), s == 3)
+                        for s in range(4) for z in range(4)]
+            for c0, n, out, rc, stop in sets:
+                wait(q, *[tok[o] for o in ready(op) if o[3] < c0 + n and o[3] + o[4] > c0])
+                ins = P.matmul(out, gb[:, c0:c0 + n], T.R[:, rc:rc + 32], False, stop)
+        elif kind == "S":
+            wait(q, vpat, *deps)
+            ins = V.tensor_tensor_scan(sc[:], T.pat[:], ps[:, 0:128], 0.0, Op.add, Op.min)
+        elif kind == "T":
+            wait(q, *deps)
+            ins = V.transpose(tt[:], sc[:, 3::4])
+        else:
+            wait(q, *deps)
+            ins = V.tensor_scalar(off[:], tt[:] if k == 4 else sc[:, 3::4], HALF, None, Op.add)
+        tok[op] = done(q, ins)
+
+    todo = {"A": list(ORDER_A), "V": list(ORDER_V), "P": [("P",) + o for o in ORDER_P]}
+    while any(todo.values()):
+        moved = False
+        for q in "AVP":
+            while todo[q] and all(d in tok for d in ready(todo[q][0])):
+                emit(q, todo[q].pop(0))
+                moved = True
+        assert moved
+
+    for c in range(3):
+        r = chunk_rank[c]
+        wait("G", *[tok[o] for o in allG if o[1] == c and o[2] == 5])
+        rid, pid, _ = topo.addr(cores[r])
+        g.remote_dma(T.ui[:, K * me:K * me + K], T.uo[:, K * r:K * r + K], S["qu%d" % me], S.left, pid, rid, bits(eng[r][1]))
+        left[0] += len(eng[r][1])
+
+    own = [o for o in allG if o[1] == 3 and o[2] == 5]
+    seq = [1, 0, 2, 3] if me == 0 else [0, 1, 2, 3]
+    at = seq.index(me)
+    fin = {}
+    for n, h in [(n, h) for n in range(at) for h in range(2)] + [(n, h) for h in range(2) for n in range(at, N)]:
+        q = seq[n]
+        if q == me:
+            wait("P", *[tok[o] for o in own if o[3] < 256 * h + 256 and o[3] + o[4] > 256 * h])
+        else:
+            wait("P", ("qu%d" % q, len(came[q][1])))
+        ins = P.matmul(pb[4 + h][:, 0:256], T.Irep[:, 0:128], T.ui[:, K * q + 256 * h:K * q + 256 * h + 256], n == 0, n == N - 1)
+        if n == N - 1:
+            fin[h] = done("P", ins)
+    wait("A", fin[0])
+    a = done("A", A.activation(T.ysb[:, 0:256], pb[4][:, 0:256], Act.Copy))
+    wait("V", fin[1])
+    v = done("V", V.tensor_copy(T.ysb[:, 256:512], pb[5][:, 0:256]))
+    wait("A", a)
+    A.dma_start(T.y[:, 0:256], T.ysb[:, 0:256]).then_inc(S.st0, 16)
+    wait("Y", v)
+    Y.dma_start(T.y[:, 256:512], T.ysb[:, 256:512]).then_inc(S.st1, 16)
+
+    wait("G", ("left", left[0]), ("sV", count["V"]), ("sA", count["A"]), ("sP", count["P"]), ("sG", count["G"]),
+         ("st0", 16), ("st1", 16))

@@ -3,38 +3,119 @@ from concourse.mybir import AluOpType as Op, ActivationFunctionType as Act
 
 N, L, K = 4, 4096, 512
 HALF = 2048.0
-BIG = 32768.0
 
 SCRATCH = {
     "Si": ("sbuf", [128, 96], "int32"), "Pl": ("sbuf", [128, 32], "int32"), "tz": ("sbuf", [128, 32], "int32"),
-    "Sh": ("sbuf", [128, 96], "float16"),
-    "offq": ("sbuf", [128, N * 32], "uint16"),
-    "WA": ("sbuf", [128, N * 128], "float16"), "WZ": ("sbuf", [128, N * 128], "float16"),
-    "tr0": ("sbuf", [128, 256], "int32"), "tr1": ("sbuf", [128, 256], "int32"),
-    "xi0": ("sbuf", [128, 256], "int32"), "xi1": ("sbuf", [128, 256], "int32"),
-    "xh0": ("sbuf", [128, 256], "float16"), "xh1": ("sbuf", [128, 256], "float16"),
+    "Sh": ("sbuf", [128, 96], "float16"), "Ip": ("sbuf", [128, 384], "float16"),
+    "off": ("sbuf", [128, 32 * 20], "uint16"), "W": ("sbuf", [128, N * 256], "float16"),
+    "tr": ("sbuf", [128, 512], "int32"), "xi": ("sbuf", [128, 512], "int32"), "xh": ("sbuf", [128, 512], "float16"),
     "win": ("sbuf", [128, L], "float32"), "U": ("sbuf", [128, L], "bfloat16"),
+    "gb": ("sbuf", [128, 512 * 16], "float16"), "sc": ("sbuf", [128, 128 * 16], "float32"),
+    "tt": ("sbuf", [128, 32 * 16], "float32"),
     "uo": ("sbuf", [128, N * K], "bfloat16"), "ui": ("sbuf", [128, N * K], "bfloat16"),
     "ysb": ("sbuf", [128, K], "float32"),
-    "V": ("sbuf", [128, 352], "int32"), "Vm": ("sbuf", [128, 64], "int32"), "J": ("sbuf", [128, 64], "float32"),
-    "Ip": ("sbuf", [128, 384], "float16"), "Irep": ("sbuf", [128, 1024], "bfloat16"),
+    "V": ("sbuf", [128, 320], "int32"), "J": ("sbuf", [128, 64], "float16"),
+    "Irep": ("sbuf", [128, 1024], "bfloat16"),
     "R": ("sbuf", [128, 320], "float16"), "RC": ("sbuf", [128, 256], "float16"),
-    "wk": ("sbuf", [128, 4], "float32"), "pat": ("sbuf", [128, 128], "float32"),
+    "pat": ("sbuf", [128, 128], "float32"),
 }
-for _c in range(N):
-    SCRATCH["gb%d" % _c] = ("sbuf", [128, K], "float16")
-    SCRATCH["sc%d" % _c] = ("sbuf", [128, 128], "float32")
-    SCRATCH["tt%d" % _c] = ("sbuf", [128, 32], "float32")
-    SCRATCH["off%d" % _c] = ("sbuf", [128, 32], "uint16")
 for _b in range(8):
     SCRATCH["pb%d" % _b] = ("psum", [128, 512], "float32")
 
-SEMAPHORES = (["sV", "sA", "sP", "sG", "lw", "lp", "lt0", "lt1", "ls0", "ls1", "acc", "left", "st0", "st1"]
-              + ["%s%d" % (n, q) for n in ("qo", "qa", "qz", "qu") for q in range(N)])
+SEMAPHORES = (["sV", "sA", "sP", "sG", "lw", "lp", "lt0", "lt1", "lt2", "ls", "acc", "left", "st"]
+              + ["%s%d" % (n, q) for n in ("qo", "qw", "qz", "qu", "qv") for q in range(N)])
 
-ORDER_A = [('G', 3, 1, 192, 320), ('G', 0, 1, 128, 384), ('G', 1, 1, 0, 512), ('G', 0, 2, 0, 256), ('G', 2, 2, 0, 384), ('G', 1, 2, 0, 384), ('G', 0, 3, 0, 320), ('G', 2, 3, 0, 512), ('G', 1, 3, 256, 256), ('G', 0, 4, 0, 192), ('G', 3, 2, 0, 384), ('G', 1, 4, 0, 448), ('G', 0, 5, 256, 256), ('G', 2, 4, 0, 512), ('G', 3, 3, 320, 192), ('G', 1, 5, 0, 512), ('G', 2, 5, 256, 256), ('G', 3, 4, 0, 256), ('G', 3, 5, 0, 256)]
-ORDER_V = [('G', 2, 1, 0, 512), ('G', 0, 1, 0, 128), ('G', 3, 1, 0, 192), ('S', 2, 1), ('S', 0, 1), ('C', 0, 1), ('C', 2, 1), ('G', 0, 2, 256, 256), ('S', 1, 1), ('G', 2, 2, 384, 128), ('C', 1, 1), ('S', 0, 2), ('S', 3, 1), ('C', 0, 2), ('G', 1, 2, 384, 128), ('S', 2, 2), ('G', 0, 3, 320, 192), ('C', 2, 2), ('C', 3, 1), ('S', 1, 2), ('S', 0, 3), ('C', 1, 2), ('C', 0, 3), ('G', 1, 3, 0, 256), ('G', 0, 4, 192, 320), ('S', 1, 3), ('G', 3, 2, 384, 128), ('C', 1, 3), ('S', 0, 4), ('S', 2, 3), ('T', 0, 4), ('G', 1, 4, 448, 64), ('C', 0, 4), ('C', 2, 3), ('G', 0, 5, 0, 256), ('S', 1, 4), ('S', 3, 2), ('T', 1, 4), ('C', 3, 2), ('C', 1, 4), ('G', 3, 3, 0, 320), ('S', 2, 4), ('T', 2, 4), ('C', 2, 4), ('S', 3, 3), ('G', 2, 5, 0, 256), ('C', 3, 3), ('G', 3, 4, 256, 256), ('S', 3, 4), ('T', 3, 4), ('C', 3, 4), ('G', 3, 5, 256, 256)]
-ORDER_P = [(2, 1), (0, 1), (3, 1), (1, 1), (0, 2), (2, 2), (1, 2), (0, 3), (2, 3), (1, 3), (0, 4), (3, 2), (1, 4), (2, 4), (3, 3), (3, 4)]
+CFG = {"pieces": [(0, 256), (256, 256)], "wcalls": 2, "gc": 1.5, "deal": {"sync": 220, "latp": 220},
+       "V": "zIp zRC zW I J RC0 RC1 RC2 RC3 x y T X0 Y0 X1 Y1 off R W e1 e3 e5 e7",
+       "A": "I2 Ip I4 ht hxy I8 h0 t0 t1 h1 t2 e0 e2 e4 e6 t3 nR",
+       "P": "W0 W1 W2 p0 p1",
+       "slots": "31 01 11 21 32 02 12 22 33 03 13 23 04 14 24 34 05 15a 25a 15b 25b 35",
+       "sends": [[(0, 1, 0, 512)], [(1, 1, 0, 256), (2, 1, 0, 256)], [(1, 1, 256, 256), (2, 1, 256, 256)]],
+       "late": [0, 3, 1, 2], "pre": [0, 3], "fin": [(0, 128, "V"), (128, 128, "A"), (256, 128, "V"), (384, 128, "A")]}
+
+
+def meet(a, n, b, m):
+    return a < b + m and b < a + n
+
+
+def deal(s, gc, fv=60, fa=78, sync=108, pe=0.5, latp=170, q=64, minp=128, look=0.6):
+    sl = [(int(w[0]), int(w[1])) + {"": (0, K), "a": (0, K // 2), "b": (K // 2, K // 2)}[w[2:]] for w in s.split()]
+    n = len(sl)
+    lo, hi = [x[2] for x in sl], [x[2] + x[3] for x in sl]
+    gend = [[] for _ in sl]
+    need = [[j for j in range(n) if sl[j][:2] == (x[0], x[1] - 1) and (x[1] == 5 or meet(*x[2:], *sl[j][2:]))] for x in sl]
+    made, small, sdone, rank, pdone = {}, {}, {}, {}, set()
+    st, out = {"A": 0.0, "V": 0.0, "P": 0.0}, {"A": [], "V": []}
+
+    def cost(o):
+        return fv + (max(64, sl[o[1]][3] // 4) if o[0] == "S" else 64)
+
+    def lready(i):
+        if sl[i][1] == 5:
+            return made.get(max(need[i]))
+        return max([made[j] for j in need[i]], default=0.0) if all(j in made for j in need[i]) else None
+
+    def give(qn, i, c0, take, t):
+        o = ("G", i, c0, take)
+        out[qn].append(o)
+        st[qn] = rank[o] = t + (fa if qn == "A" else fv) + take * gc
+        gend[i].append((c0, take, st[qn]))
+        for j, (c, k, a0, sn) in enumerate(sl):
+            if k >= 5 or j in pdone:
+                continue
+            if hi[j] > lo[j]:
+                return
+            t, m = st["P"] + sn / 4 * pe, 128 if k % 2 else 32
+            for e in sorted(max(e for a, b, e in gend[j] if meet(a, b, c1, m)) for c1 in range(a0, a0 + sn, m)):
+                t = max(t, e + sync) + (64 if k % 2 else 32) * pe
+            st["P"] = t
+            pdone.add(j)
+            small[("S", j)] = t + latp
+
+    while any(hi[i] > lo[i] for i in range(n)) or small:
+        i = next((i for i in range(n) if hi[i] > lo[i]), None)
+        lr = lready(i) if i is not None else None
+        tA, tV = st["A"], st["V"]
+        if tA <= tV and lr is not None and (max(tA, lr) <= tV or not small):
+            t = max(tA, lr)
+            left = take = hi[i] - lo[i]
+            if left > minp:
+                busy = sum(cost(o) for o, r in small.items() if r < t + left * gc * look)
+                want = (max(tV, lr) + busy - t + left * gc) / (2 * gc)
+                take = max(minp, min(left, int(round(want / q)) * q))
+                if left - take < 64:
+                    take = left
+            hi[i] -= take
+            give("A", i, hi[i], take, t)
+            continue
+        rdy = sorted((r, o) for o, r in small.items())
+        if rdy and (rdy[0][0] <= tV or lr is None or rdy[0][0] <= max(tV, lr) + 30):
+            o = min((o for r, o in rdy if r <= max(tV, rdy[0][0])), key=lambda o: o[1])
+            tV = st["V"] = max(tV, small.pop(o)) + cost(o)
+            out["V"].append(o)
+            c, k = sl[o[1]][:2]
+            if o[0] == "S":
+                sdone[o[1]] = tV
+                js = [j for j in range(n) if sl[j][:2] == (c, 4)]
+                if k < 4:
+                    small[("C", o[1])] = tV + sync
+                elif all(j in sdone for j in js):
+                    small[("T", max(js))] = tV + sync
+            elif o[0] == "T":
+                small[("D", o[1])] = tV + sync
+            else:
+                made[o[1]] = tV + sync
+            continue
+        t = max(tV, lr)
+        take = left = hi[i] - lo[i]
+        if left == sl[i][3]:
+            want = (max(tA, lr) - t + left * gc) / (2 * gc)
+            if rdy:
+                want = min(want, max(64, (rdy[0][0] - t) / gc))
+            take = max(64, min(left, int(round(want / q)) * q))
+        lo[i] += take
+        give("V", i, lo[i] - take, take, t)
+    return sl, out["A"], out["V"], rank
 
 
 def peers_of(cores, me, topo):
@@ -50,12 +131,12 @@ def engine_sets(cores, me, topo):
     for n, r in enumerate(far):
         e = topo.engines(c, cores[r])
         part = len(e) // len(far)
-        out[r] = (e[n * part:(n + 1) * part], e)
+        out[r] = (e[n * part:(n + 1) * part], e, e)
         used |= set(e)
     for r in peers_of(cores, me, topo):
         if r not in far:
             e = [x for x in topo.engines(c, cores[r]) if x not in used]
-            out[r] = (e, e)
+            out[r] = (e, e, topo.engines(c, cores[r]))
     return out
 
 
@@ -73,10 +154,11 @@ def rank_program(g, core, T, topo):
     chunk_rank = peers + [me]
     eng = engine_sets(cores, me, topo)
     came = {q: engine_sets(cores, q, topo)[me] for q in peers}
+    back = {r: peers_of(cores, r, topo).index(me) for r in peers}
 
     Q = {"V": g.vector, "A": g.scalar, "P": g.tensor, "G": g, "Y": g.sync}
     count = {"V": 0, "A": 0, "P": 0, "G": 0}
-    seen = {}
+    seen, tok = {}, {}
 
     def done(q, ins):
         count[q] += 1
@@ -89,238 +171,242 @@ def rank_program(g, core, T, topo):
                 Q[q].wait_ge(S[name], val)
                 seen[(q, name)] = val
 
+    def run(todo, ready, emit):
+        while any(todo.values()):
+            moved = False
+            for q in todo:
+                while todo[q] and all(d in tok for d in ready(todo[q][0])):
+                    op = todo[q].pop(0)
+                    tok[op] = emit(q, op)
+                    moved = True
+            assert moved, todo
+
     V, A, P, Y = g.vector, g.scalar, g.tensor, g.sync
+
+    def copy(q, dst, src, add=None):
+        if q == "V":
+            return V.tensor_copy(dst, src) if add is None else V.tensor_scalar(dst, src, add, None, Op.add)
+        return A.activation(dst, src, Act.Copy) if add is None else A.activation(dst, src, Act.Identity, bias=add)
+
     pb = [T["pb%d" % b] for b in range(8)]
-    mine = slice(128 * me, 128 * me + 128)
+    mine = slice(256 * me, 256 * me + 256)
+    pieces = CFG["pieces"]
 
-    Y.dma_start(T.Si[:, 0:32], T.when[:]).then_inc(S.lw, 16)
     A.dma_start(T.Pl[:], T.place[:]).then_inc(S.lp, 16)
-    for h in range(2):
-        for xy in range(2):
-            (Y, A)[xy].dma_start(T["tr%d" % h][64 * xy:64 * xy + 64, :],
-                                 T.track[:, 2048 * h:2048 * h + 2048]).then_inc(S["lt%d" % h], 16)
-    Y.dma_start(T.U[:, 0:2048], T.sound[:, 0:2048]).then_inc(S.ls0, 16)
+    Y.dma_start(T.Si[:, 0:32], T.when[:]).then_inc(S.lw, 16)
+    for h, (c0, n) in enumerate(pieces):
+        (Y, A)[h % 2].dma_start(T.tr[0:64, c0:c0 + n], T.track[:, 8 * c0:8 * (c0 + n)]).then_inc(S["lt%d" % h], 16)
+        tok["lt%d" % h] = ("lt%d" % h, 16)
+    Y.dma_start(T.U[:], T.sound[:]).then_inc(S.ls, 16)
+    tok.update(lw=("lw", 16), lp=("lp", 16))
 
-    gI = done("G", g.iota(T.V[:, 0:128], [[1, 128]], 0, -1))
-    done("G", g.iota(T.V[:, 288:320], [[1, 4], [4, 4], [16, 2]], 128, -1))
-    gC = done("G", g.iota(T.V[:, 320:352], [[1, 32]], 128, -1))
-    done("G", g.iota(T.V[:, 128:256], [[1, 8], [16, 8], [8, 2]], 0, -1))
-    done("G", g.iota(T.V[:, 256:272], [[34, 4], [16, 2], [8, 2]], 0, -1))
-    gR = done("G", g.iota(T.V[:, 272:288], [[34, 4], [16, 2], [8, 2]], 1, -1))
+    tok["gI"] = done("G", g.iota(T.V[:, 32:160], [[1, 128]], 0, -1))
+    tok["gJ"] = done("G", g.iota(T.V[:, 0:32], [[1, 4], [4, 4], [16, 2]], 0, -1))
+    done("G", g.iota(T.V[:, 160:288], [[1, 8], [8, 16]], 0, -1))
+    tok["gR"] = done("G", g.iota(T.V[:, 288:320], [[1, 2], [34, 4], [8, 4]], 0, -1))
+    tok["pat"] = done("G", g.iota(T.pat[:], [[0, 32], [-32767, 4]], 16384, 0, allow_small_or_imprecise_dtypes=True))
 
-    vpz = done("V", V.memset(T.pat[:], 0.0))
-    done("V", V.memset(T.Ip[:, 0:128], 0.0))
-    done("V", V.memset(T.Ip[:, 256:384], 0.0))
-    wait("V", gI)
-    vI0 = done("V", V.tensor_scalar(T.Irep[:, 0:128], T.V[:, 0:128], 0.0, None, Op.is_equal))
-    vIp = done("V", V.tensor_scalar(T.Ip[:, 128:256], T.V[:, 0:128], 0.0, None, Op.is_equal))
-    done("V", V.memset(T.wk[0:32, :], 1.0))
-    done("V", V.memset(T.wk[32:64, 0:1], 1.0))
-    done("V", V.memset(T.wk[32:64, 1:2], -1.0))
-    done("V", V.memset(T.wk[32:64, 2:4], 0.0))
-    wait("V", gC)
-    vm = done("V", V.tensor_scalar(T.Vm[0:96, :], T.V[0:96, 288:352], 31, None, Op.bitwise_and))
-    done("V", V.memset(T.wk[64:96, 0:2], 0.0))
-    done("V", V.memset(T.wk[64:96, 2:3], 1.0))
-    done("V", V.memset(T.wk[64:96, 3:4], -1.0))
-    wait("V", vpz, vm)
-    vpat = done("V", V.memset(T.pat[:, 0::4], BIG))
-    vJ = done("V", V.tensor_scalar(T.J[0:96, :], T.Vm[0:96, :], 0.0, None, Op.is_equal))
-    wait("V", gR)
-    vR = done("V", V.tensor_scalar(T.R[:, 1::2], T.V[:, 128:288], 0.0, None, Op.is_equal))
+    def equal(dst, src, val=0.0, times=None):
+        if times is None:
+            return V.tensor_scalar(dst, src, val, None, Op.is_equal)
+        return V.tensor_scalar(dst, src, val, times, Op.is_equal, Op.mult)
 
-    wait("A", vI0)
-    a = done("A", A.activation(T.Irep[:, 128:256], T.Irep[:, 0:128], Act.Copy))
-    done("A", A.activation(T.WA[96:128, mine], T.Irep[96:128, 0:128], Act.Copy))
-    wait("A", a)
-    a = done("A", A.activation(T.Irep[:, 256:512], T.Irep[:, 0:256], Act.Copy))
-    aW = done("A", A.activation(T.WZ[96:128, mine], T.Irep[96:128, 0:128], Act.Copy))
-    wait("A", a)
-    aI = done("A", A.activation(T.Irep[:, 512:1024], T.Irep[:, 0:512], Act.Copy))
-    wait("A", vJ)
-    for k in range(4):
-        done("A", A.activation(T.RC[0:96, k::4], T.J[0:96, :], Act.Identity, scale=T.wk[0:96, k:k + 1]))
-    wait("A", vR)
-    aR = done("A", A.activation(T.R[:, 0::2], T.R[:, 1::2], Act.Identity, scale=-1.0))
-
-    wait("V", ("lw", 16))
-    v1 = done("V", V.transpose(T.tz[:], T.Si[:, 0:32]))
-    wait("V", ("lp", 16))
-    done("V", V.tensor_scalar(T.Si[:, 32:64], T.Pl[:], 12, None, Op.logical_shift_right))
-    v2 = done("V", V.tensor_scalar(T.Si[:, 64:96], T.Pl[:], 4095, None, Op.bitwise_and))
-    wait("V", v1)
-    vOff = done("V", V.tensor_copy(T.offq[:, 32 * me:32 * me + 32], T.tz[:]))
-    wait("V", v2)
-    vSh = done("V", V.tensor_scalar(T.Sh[:], T.Si[:], -HALF, None, Op.add))
-
-    ax = {}
-    for h in range(2):
-        tr, xi, xh = T["tr%d" % h], T["xi%d" % h], T["xh%d" % h]
-        wait("V", ("lt%d" % h, 32))
-        done("V", V.tensor_scalar(xi[0:64, :], tr[0:64, :], 12, None, Op.logical_shift_right))
-        a = done("V", V.tensor_scalar(xi[64:128, :], tr[64:128, :], 4095, None, Op.bitwise_and))
-        wait("A", a)
-        ax[h] = done("A", A.activation(xh[:], xi[:], Act.Identity, bias=-HALF))
-
-    wait("P", vIp, vSh)
-    for q in range(3):
+    def table(q):
+        rows = slice(32 * q, 32 * q + 32)
         for il in range(8):
-            o = pb[7][32 * q:32 * q + 32, 16 * il:16 * il + 16]
+            o = pb[7][rows, 16 * il:16 * il + 16]
             P.matmul(o, T.Ip[:, 128 + il:384:8], T.Sh[:, 32 * q:32 * q + 16], True, False)
-            ins = P.matmul(o, T.Ip[:, il:256:8], T.Sh[:, 32 * q + 16:32 * q + 32], False, True)
-    pWA = done("P", ins)
-    for q in range(3):
+            P.matmul(o, T.Ip[:, il:256:8], T.Sh[:, 32 * q + 16:32 * q + 32], False, True)
         for z in range(4):
-            ins = P.matmul(pb[6][32 * q:32 * q + 32, 32 * z:32 * z + 32], T.Ip[:, 128 + 32 * z:160 + 32 * z],
-                           T.Sh[:, 32 * q:32 * q + 32], True, True)
-    pWZ = done("P", ins)
-    wait("V", pWA)
-    vWA = done("V", V.tensor_copy(T.WA[0:96, mine], pb[7][0:96, 0:128]))
-    wait("V", pWZ)
-    vWZ = done("V", V.tensor_copy(T.WZ[0:96, mine], pb[6][0:96, 0:128]))
+            ins = P.matmul(pb[7][rows, 128 + 32 * z:160 + 32 * z], T.Ip[:, 128 + 32 * z:160 + 32 * z], T.Sh[:, rows], True, True)
+        return ins
 
-    bank = {}
-    for h in range(2):
-        wait("P", ax[h], aI)
+    def spread(h):
+        c0, n = pieces[h]
         for k in range(8):
-            b = 4 * h + k // 2
-            if b >= 6:
-                wait("P", vWZ)
-            ins = P.matmul(pb[b][:, 256 * (k % 2):256 * (k % 2) + 256], T.Irep[:, k::8], T["xh%d" % h][:], True, True)
-            if k % 2:
-                bank[b] = done("P", ins)
-    for b in (1, 3, 5, 7):
-        wait("A", bank[b])
-        winA = done("A", A.activation(T.win[:, 512 * b:512 * b + 512], pb[b][:], Act.Copy))
-    for b in (0, 2, 4, 6):
-        wait("V", bank[b])
-        winV = done("V", V.tensor_copy(T.win[:, 512 * b:512 * b + 512], pb[b][:]))
-        if b == 0:
-            wait("Y", winV)
-            Y.dma_start(T.U[:, 2048:4096], T.sound[:, 2048:4096]).then_inc(S.ls1, 16)
+            w0, j = 8 * c0 + k * n, 0
+            while j < n:
+                b, o = (w0 + j) // 512, (w0 + j) % 512
+                m = min(n - j, 512 - o)
+                if b == 7:
+                    wait("P", tok["W"])
+                ins = P.matmul(pb[b][:, o:o + m], T.Irep[:, k::8], T.xh[:, c0 + j:c0 + j + m], True, True)
+                j += m
+                if o + m == 512 and (k < 7 or j < n):
+                    tok["b%d" % b] = done("P", ins)
+        return ins
+
+    start = {
+        "zIp": ("", lambda q: V.memset(T.Ip[:], 0.0)),
+        "zRC": ("", lambda q: V.memset(T.RC[0:96, :], 0.0)),
+        "zW": ("", lambda q: V.memset(T.W[96:128, mine], 0.0)),
+        "I": ("gI", lambda q: equal(T.Irep[:, 0:128], T.V[:, 32:160])),
+        "Ip": ("I zIp", lambda q: copy(q, T.Ip[:, 128:256], T.Irep[:, 0:128])),
+        "I2": ("I", lambda q: copy(q, T.Irep[:, 128:256], T.Irep[:, 0:128])),
+        "I4": ("I2", lambda q: copy(q, T.Irep[:, 256:512], T.Irep[:, 0:256])),
+        "I8": ("I4", lambda q: copy(q, T.Irep[:, 512:1024], T.Irep[:, 0:512])),
+        "J": ("gJ", lambda q: equal(T.J[0:32, :], T.V[0:32, 0:64])),
+        "R": ("gR", lambda q: equal(T.R[:, 1::2], T.V[:, 160:320])),
+        "nR": ("R", lambda q: A.activation(T.R[:, 0::2], T.R[:, 1::2], Act.Identity, scale=-1.0) if q == "A"
+               else equal(T.R[:, 0::2], T.V[:, 160:320], 0.0, -1.0)),
+        "x": ("lp", lambda q: V.tensor_scalar(T.Si[:, 32:64], T.Pl[:], 12, None, Op.logical_shift_right)),
+        "y": ("lp", lambda q: V.tensor_scalar(T.Si[:, 64:96], T.Pl[:], 4095, None, Op.bitwise_and)),
+        "ht": ("lw", lambda q: copy(q, T.Sh[:, 0:32], T.Si[:, 0:32], -HALF)),
+        "hxy": ("x y", lambda q: copy(q, T.Sh[:, 32:96], T.Si[:, 32:96], -HALF)),
+        "T": ("lw", lambda q: V.transpose(T.tz[:], T.Si[:, 0:32])),
+        "off": ("T", lambda q: copy(q, T.off[:, 96:128], T.tz[:])),
+        "W": ("W0 W1 W2", lambda q: copy(q, T.W[0:96, mine], pb[7][0:96, 0:256])),
+    }
+    for n in range(4):
+        p = 32 + 32 * (n // 2)
+        start["RC%d" % n] = ("gJ zRC", lambda q, n=n, p=p: equal(T.RC[p:p + 32, n::4], T.V[p:p + 32, 0:64], -float(p), 1.0 - 2.0 * (n % 2)))
+        start["t%d" % n] = ("J zRC", lambda q, n=n: copy(q, T.RC[0:32, n::4], T.J[0:32, :]))
+    for n in range(3):
+        start["W%d" % n] = ("Ip hxy" if n else "Ip ht", lambda q, n=n: table(n))
+    for h, (c0, n) in enumerate(pieces):
+        c = slice(c0, c0 + n)
+        start["X%d" % h] = ("lt%d" % h, lambda q, c=c: V.tensor_scalar(T.xi[0:64, c], T.tr[0:64, c], 12, None, Op.logical_shift_right))
+        start["Y%d" % h] = ("lt%d" % h, lambda q, c=c: V.tensor_scalar(T.xi[64:128, c], T.tr[0:64, c], 4095, None, Op.bitwise_and))
+        start["h%d" % h] = ("X%d Y%d" % (h, h), lambda q, c=c: copy(q, T.xh[:, c], T.xi[:, c], -HALF))
+        last = 8 * (c0 + n) // 512 - 1
+        start["p%d" % h] = ("I8 h%d" % h, lambda q, h=h: spread(h))
+        for b in range(8 * c0 // 512, last + 1):
+            start["e%d" % b] = ("b%d" % b if b < last else "p%d" % h,
+                                lambda q, b=b: copy(q, T.win[:, 512 * b:512 * b + 512], pb[b][:]))
+
+    def begin(q, name):
+        wait(q, *[tok[d] for d in start[name][0].split()])
+        return done(q, start[name][1](q))
+
+    run({q: CFG[q].split() for q in "VAP"},
+        lambda name: start[name][0].split() + (["W"] if name == "p%d" % (len(pieces) - 1) else []), begin)
+    window = [tok["e%d" % b] for b in range(8)]
+    consts = [tok[n] for n in ("R", "nR", "RC0", "RC1", "RC2", "RC3", "t0", "t1", "t2", "t3")]
 
     left = [0]
 
-    def to_all(name, width, sem):
+    def send(items):
         tr = []
-        for r in peers:
+        for r, e, sem, src, dst in items:
             rid, pid, _ = topo.addr(cores[r])
-            ap = T[name][:, width * me:width * me + width]
-            tr.append(RemoteDMATransfer(dst_ids=[DstId(rid=rid, pnc=pid)], dma_engine_mask=bits(eng[r][0]),
-                                        remote_sem=S["%s%d" % (sem, me)], src=ap, dst=ap))
-            left[0] += len(eng[r][0])
+            tr.append(RemoteDMATransfer(dst_ids=[DstId(rid=rid, pnc=pid)], dma_engine_mask=bits(eng[r][e]),
+                                        remote_sem=S[sem % me], src=src, dst=dst))
+            left[0] += len(eng[r][e])
         g.remote_dma_fused(tr, local_sem=S.left)
 
-    wait("G", vOff)
-    to_all("offq", 32, "qo")
-    wait("G", aW, vWA)
-    to_all("WA", 128, "qa")
-    wait("G", vWZ)
-    to_all("WZ", 128, "qz")
-    wait("G", ("ls0", 16))
-    g.dma_start(T.U[:, 0:2048], T.sound[:, 1:2049], accum_op=Op.add, max_dma_last_dim=4096).then_inc(S.acc, 16)
-    wait("G", ("ls1", 16))
-    g.dma_start(T.U[:, 2048:4095], T.sound[:, 2049:4096], accum_op=Op.add, max_dma_last_dim=4096).then_inc(S.acc, 16)
+    wait("G", tok["off"])
+    send([(r, 0, "qo%d", T.off[:, 96:128], T.off[:, 32 * back[r]:32 * back[r] + 32]) for r in peers])
+    wait("G", tok["zW"], tok["W"])
+    for n in range(CFG["wcalls"]):
+        w = 256 // CFG["wcalls"]
+        ap = T.W[:, 256 * me + w * n:256 * me + w * n + w]
+        send([(r, 0, ("qw%d", "qz%d")[n], ap, ap) for r in peers])
+    wait("G", ("ls", 16))
+    g.dma_start(T.U[:, 0:L - 1], T.sound[:, 1:L], accum_op=Op.add, max_dma_last_dim=4096).then_inc(S.acc, 16)
 
-    tok = {}
-    allG = [o for o in ORDER_A + ORDER_V if o[0] == "G"]
+    slots, order_A, order_V, rank = CFG["plan"] if "plan" in CFG else deal(CFG["slots"], CFG["gc"], **CFG["deal"])
+    place = {}
+    for c, k, _, _ in slots:
+        if k < 5 and (c, k) not in place:
+            place[(c, k)] = len(place)
+    lst = {(c, 1): 32 * c for c in range(N)}
+    lst.update({(c, k + 1): 128 + 32 * place[(c, k)] for c, k in place})
+    last_read = {}
+    allG = [o for o in order_A + order_V if o[0] == "G"]
+    order_P = [("P", i) for i, sl in enumerate(slots) if sl[1] < 5]
 
     def ready(op):
-        kind, c, k = op[:3]
+        kind, i = op[:2]
+        c, k = slots[i][:2]
         if kind == "G":
-            return [("C", c, k - 1)] if k > 1 else []
+            if k == 5:
+                return [("D", max(j for j, sl in enumerate(slots) if sl[:2] == (c, 4)))]
+            return [("C", j) for j, sl in enumerate(slots) if sl[:2] == (c, k - 1) and meet(*op[2:], *sl[2:])]
         if kind == "P":
-            return [o for o in allG if o[1] == c and o[2] == k]
-        if kind == "S":
-            return [("P", c, k)]
+            return [o for o in allG if o[1] == i]
         if kind == "T":
-            return [("S", c, k)]
-        return [("T" if k == 4 else "S", c, k)]
+            return [("S", j) for j, sl in enumerate(slots) if sl[:2] == (c, 4)]
+        return [({"S": "P", "C": "S", "D": "T"}[kind], i)]
 
     def emit(q, op):
-        kind, c, k = op[:3]
-        r = chunk_rank[c]
-        gb, sc, tt, off, ps = T["gb%d" % c], T["sc%d" % c], T["tt%d" % c], T["off%d" % c], pb[c]
+        kind, i = op[:2]
         deps = [tok[d] for d in ready(op)]
+        c, k, first, cols = slots[i]
+        r, ps = chunk_rank[c], pb[i % 4]
         if kind == "G":
-            c0, n = op[3:]
+            c0, n = op[2:]
             if k == 1:
-                wait(q, winA, winV, vOff if r == me else ("qo%d" % r, len(came[r][0])))
-                lst = T.offq[:, 32 * r + c0 // 16:32 * r + (c0 + n) // 16]
-            else:
-                lst = off[:, c0 // 16:(c0 + n) // 16]
+                wait(q, *window, tok["off"] if r == me else ("qo%d" % r, len(came[r][0])))
             wait(q, *deps)
+            offs = T.off[:, lst[(c, k)] + c0 // 16:lst[(c, k)] + (c0 + n) // 16]
             if k == 5:
-                wait(q, ("acc", 32))
-                src = T.U[:, :].indirect(lst)
-                dst = (T.ui if r == me else T.uo)[:, K * r + c0:K * r + c0 + n]
-            else:
-                src = T.win[:, :].indirect(lst)
-                dst = gb[:, c0:c0 + n]
-            ins = V.tensor_copy(dst, src) if q == "V" else A.activation(dst, src, Act.Copy)
-        elif kind == "P":
-            if k == 1:
-                wait(q, winA, winV, aR, vWA if r == me else ("qa%d" % r, len(came[r][0])))
-            else:
-                wait(q, tok[("S", c, k - 1)], vWZ if r == me else ("qz%d" % r, len(came[r][0])))
-            tab, lay = (T.WA, 0) if k % 2 else (T.WZ, 128)
-            P.matmul(ps[:, 0:128], tab[0:96, 128 * r:128 * r + 128], T.RC[0:96, lay:lay + 128], True, False)
+                wait(q, ("acc", 16))
+                return done(q, copy(q, (T.ui if r == me else T.uo)[:, K * c + c0:K * c + c0 + n], T.U[:, :].indirect(offs)))
+            return done(q, copy(q, T.gb[:, K * place[(c, k)] + c0:K * place[(c, k)] + c0 + n], T.win[:, :].indirect(offs)))
+        if kind == "P":
+            wait(q, *window, *consts, *last_read.get(i % 4, []))
+            lay, g0, a, b = (0 if k % 2 else 128), K * place[(c, k)], first // 4, (first + cols) // 4
+            wait(q, tok["W"] if r == me else (("qw%d" if k == 1 or CFG["wcalls"] == 1 else "qz%d") % r, len(came[r][0])))
+            P.matmul(ps[:, a:b], T.W[0:96, 256 * r + lay:256 * r + lay + 128], T.RC[0:96, lay + a:lay + b], True, False)
+            ss = range(first // 128, (first + cols) // 128)
             if k % 2:
-                sets = [(128 * s, 128, ps[:, 32 * s:32 * s + 32], 256 + 32 * (s // 2), s == 3) for s in range(4)]
+                sets = [(128 * s, 128, ps[:, 32 * s:32 * s + 32], 256 + 32 * (s // 2)) for s in ss]
             else:
-                sets = [(128 * s + 32 * z, 32, ps[32 * z:32 * z + 32, 32 * s:32 * s + 32], 32 * (2 * z + s // 2), s == 3)
-                        for s in range(4) for z in range(4)]
-            for c0, n, out, rc, stop in sets:
-                wait(q, *[tok[o] for o in ready(op) if o[3] < c0 + n and o[3] + o[4] > c0])
-                ins = P.matmul(out, gb[:, c0:c0 + n], T.R[:, rc:rc + 32], False, stop)
-        elif kind == "S":
-            wait(q, vpat, *deps)
-            ins = V.tensor_tensor_scan(sc[:], T.pat[:], ps[:, 0:128], 0.0, Op.add, Op.min)
-        elif kind == "T":
-            wait(q, *deps)
-            ins = V.transpose(tt[:], sc[:, 3::4])
+                sets = [(128 * s + 32 * z, 32, ps[32 * z:32 * z + 32, 32 * s:32 * s + 32], 32 * (2 * z + s // 2))
+                        for s in ss for z in range(4)]
+            gs = sorted(ready(op), key=lambda o: rank[o])
+            sets.sort(key=lambda st: max(n for n, o in enumerate(gs) if meet(*o[2:], *st[:2])))
+            for n, (c0, m, out, rc) in enumerate(sets):
+                wait(q, *[tok[o] for o in gs if meet(*o[2:], c0, m)])
+                ins = P.matmul(out, T.gb[:, g0 + c0:g0 + c0 + m], T.R[:, rc:rc + 32], False,
+                               all(st[0] % 128 != c0 % 128 for st in sets[n + 1:]))
+            return done(q, ins)
+        wait(q, tok["pat"], *deps)
+        p0 = place[(c, k)]
+        a, b = (0, 128) if kind in "TD" else (first // 4, (first + cols) // 4)
+        sc3, tt = T.sc[:, 128 * p0 + a + 3:128 * p0 + b:4], T.tt[:, 32 * p0:32 * p0 + 32]
+        if kind == "S":
+            ins = V.tensor_tensor_scan(T.sc[:, 128 * p0 + a:128 * p0 + b], T.pat[:, 0:b - a], ps[:, a:b], 0.0, Op.max, Op.min)
+            last_read[i % 4] = [done(q, ins)]
+            return last_read[i % 4][0]
+        if kind == "T":
+            return done(q, V.transpose(tt, sc3))
+        return done(q, copy(q, T.off[:, 128 + 32 * p0 + a // 4:128 + 32 * p0 + b // 4], sc3 if kind == "C" else tt, HALF))
+
+    run({"A": list(order_A), "V": list(order_V), "P": order_P}, ready, emit)
+
+    def sound_of(c, c0, m):
+        return [tok[o] for o in allG if slots[o[1]][:2] == (c, 5) and meet(*o[2:], c0, m)]
+
+    for cs in CFG["sends"]:
+        for c, e, c0, m in cs:
+            wait("G", *sound_of(c, c0, m))
+        send([(chunk_rank[c], e, "qv%d" if c0 else "qu%d", T.uo[:, K * c + c0:K * c + c0 + m],
+               T.ui[:, K * back[chunk_rank[c]] + c0:K * back[chunk_rank[c]] + c0 + m]) for c, e, c0, m in cs])
+    sent = [x for cs in CFG["sends"] for x in cs]
+
+    fin, late = CFG["fin"], CFG["late"]
+    seq = [1, 0, 2, 3] if late.index(chunk_rank.index(0)) > late.index(chunk_rank.index(1)) else [0, 1, 2, 3]
+    pre = 0
+    while pre < N - 1 and chunk_rank.index(seq[pre]) in CFG["pre"]:
+        pre += 1
+    H, summed = range(len(fin)), {}
+    for n, h in [(n, h) for n in range(pre) for h in H] + [(n, h) for h in H for n in range(pre, N)]:
+        r, (c0, m, _) = seq[n], fin[h]
+        c = chunk_rank.index(r)
+        if r == me:
+            wait("P", *sound_of(c, c0, m))
         else:
-            wait(q, *deps)
-            ins = V.tensor_scalar(off[:], tt[:] if k == 4 else sc[:, 3::4], HALF, None, Op.add)
-        tok[op] = done(q, ins)
-
-    todo = {"A": list(ORDER_A), "V": list(ORDER_V), "P": [("P",) + o for o in ORDER_P]}
-    while any(todo.values()):
-        moved = False
-        for q in "AVP":
-            while todo[q] and all(d in tok for d in ready(todo[q][0])):
-                emit(q, todo[q].pop(0))
-                moved = True
-        assert moved
-
-    for c in range(3):
-        r = chunk_rank[c]
-        wait("G", *[tok[o] for o in allG if o[1] == c and o[2] == 5])
-        rid, pid, _ = topo.addr(cores[r])
-        g.remote_dma(T.ui[:, K * me:K * me + K], T.uo[:, K * r:K * r + K], S["qu%d" % me], S.left, pid, rid, bits(eng[r][1]))
-        left[0] += len(eng[r][1])
-
-    own = [o for o in allG if o[1] == 3 and o[2] == 5]
-    seq = [1, 0, 2, 3] if me == 0 else [0, 1, 2, 3]
-    at = seq.index(me)
-    fin = {}
-    for n, h in [(n, h) for n in range(at) for h in range(2)] + [(n, h) for h in range(2) for n in range(at, N)]:
-        q = seq[n]
-        if q == me:
-            wait("P", *[tok[o] for o in own if o[3] < 256 * h + 256 and o[3] + o[4] > 256 * h])
-        else:
-            wait("P", ("qu%d" % q, len(came[q][1])))
-        ins = P.matmul(pb[4 + h][:, 0:256], T.Irep[:, 0:128], T.ui[:, K * q + 256 * h:K * q + 256 * h + 256], n == 0, n == N - 1)
+            wait("P", *[(("qv%d" if a else "qu%d") % r, len(came[r][e])) for cc, e, a, w in sent if cc == back[r] and meet(a, w, c0, m)])
+        ins = P.matmul(pb[4 + h][:, 0:m], T.Irep[:, 0:128], T.ui[:, K * c + c0:K * c + c0 + m], n == 0, n == N - 1)
         if n == N - 1:
-            fin[h] = done("P", ins)
-    wait("A", fin[0])
-    a = done("A", A.activation(T.ysb[:, 0:256], pb[4][:, 0:256], Act.Copy))
-    wait("V", fin[1])
-    v = done("V", V.tensor_copy(T.ysb[:, 256:512], pb[5][:, 0:256]))
-    wait("A", a)
-    A.dma_start(T.y[:, 0:256], T.ysb[:, 0:256]).then_inc(S.st0, 16)
-    wait("Y", v)
-    Y.dma_start(T.y[:, 256:512], T.ysb[:, 256:512]).then_inc(S.st1, 16)
+            summed[h] = done("P", ins)
+    for h, (c0, m, q) in enumerate(fin):
+        wait(q, summed[h])
+        a = done(q, copy(q, T.ysb[:, c0:c0 + m], pb[4 + h][:, 0:m]))
+        sq = "A" if h == len(fin) - 1 else "Y"
+        wait(sq, a)
+        Q[sq].dma_start(T.y[:, c0:c0 + m], T.ysb[:, c0:c0 + m]).then_inc(S.st, 16)
 
     wait("G", ("left", left[0]), ("sV", count["V"]), ("sA", count["A"]), ("sP", count["P"]), ("sG", count["G"]),
-         ("st0", 16), ("st1", 16))
+         ("st", 16 * len(fin)))

@@ -10,27 +10,29 @@ SCRATCH = {
     "off": ("sbuf", [128, 32 * 20], "uint16"), "W": ("sbuf", [128, N * 256], "float16"),
     "tr": ("sbuf", [128, 512], "int32"), "xi": ("sbuf", [128, 512], "int32"), "xh": ("sbuf", [128, 512], "float16"),
     "win": ("sbuf", [128, L], "float32"), "U": ("sbuf", [128, L], "bfloat16"),
-    "gb": ("sbuf", [128, 512 * 16], "float16"), "sc": ("sbuf", [128, 128 * 16], "float32"),
-    "tt": ("sbuf", [128, 32 * 16], "float32"),
+    "gb": ("sbuf", [128, K * 16], "float16"), "sc": ("sbuf", [128, 128 * 16], "uint16"),
     "uo": ("sbuf", [128, N * K], "bfloat16"), "ui": ("sbuf", [128, N * K], "bfloat16"),
     "ysb": ("sbuf", [128, K], "float32"),
     "V": ("sbuf", [128, 320], "int32"), "J": ("sbuf", [128, 64], "float16"),
     "Irep": ("sbuf", [128, 1024], "bfloat16"),
     "R": ("sbuf", [128, 320], "float16"), "RC": ("sbuf", [128, 256], "float16"),
-    "pat": ("sbuf", [128, 128], "float32"),
+    "pat": ("sbuf", [128, 128], "float32"), "pm": ("sbuf", [128, 256], "float16"),
 }
 for _b in range(8):
     SCRATCH["pb%d" % _b] = ("psum", [128, 512], "float32")
 
 SEMAPHORES = (["sV", "sA", "sP", "sG", "lw", "lp", "lt0", "lt1", "lt2", "ls", "acc", "left", "st"]
-              + ["%s%d" % (n, q) for n in ("qo", "qw", "qz", "qu", "qv") for q in range(N)])
+              + ["%s%d" % (n, q) for n in ("qo", "qa", "qz", "qu", "qv") for q in range(N)])
 
-CFG = {"pieces": [(0, 256), (256, 256)], "wcalls": 2, "gc": 1.5, "deal": {"sync": 220, "latp": 220},
-       "V": "zIp zRC zW I J RC0 RC1 RC2 RC3 x y T X0 Y0 X1 Y1 off R W e1 e3 e5 e7",
-       "A": "I2 Ip I4 ht hxy I8 h0 t0 t1 h1 t2 e0 e2 e4 e6 t3 nR",
-       "P": "W0 W1 W2 p0 p1",
-       "slots": "31 01 11 21 32 02 12 22 33 03 13 23 04 14 24 34 05 15a 25a 15b 25b 35",
-       "sends": [[(0, 1, 0, 512)], [(1, 1, 0, 256), (2, 1, 0, 256)], [(1, 1, 256, 256), (2, 1, 256, 256)]],
+CFG = {"pieces": [(0, 128), (128, 128), (256, 256)],
+       "V": "pm0 zIp pm1 zRC I J I2 T x y off X0 Y0 X1 Y1 X2 Y2 h1 zW e0 e2 e4 e6 RC0 RC1 RC2 RC3 cRC",
+       "A": "Ip ht I4 hxy I8 h0 t0 W h2 e1 e3 e5 e7 t1 t2",
+       "P": "W0 W1 W2 p0 p1 p2",
+       "G": "gI gJ Ra sendO sendA sendZ Rb Rc t3 pat add",
+       "share": [256, 256] + [192, 192, 224] * 4 + [192, 192], "flip": 12, "stq": "YYYA", "fuse": True,
+       "endV": "U0:384:128 D14 S15 U2:0:256 D15 U2:256:160 U3:0:256",
+       "endA": "U0:0:192 U0:192:192 U1:0:256 U1:256:256 U2:416:96 U3:256:256",
+       "sends": [[(0, 1, 0, 192)], [(0, 1, 192, 320)], [(1, 1, 0, 256), (2, 1, 0, 256)], [(1, 1, 256, 256), (2, 1, 256, 256)]],
        "late": [0, 3, 1, 2], "pre": [0, 3], "fin": [(0, 128, "V"), (128, 128, "A"), (256, 128, "V"), (384, 128, "A")]}
 
 
@@ -38,84 +40,20 @@ def meet(a, n, b, m):
     return a < b + m and b < a + n
 
 
-def deal(s, gc, fv=60, fa=78, sync=108, pe=0.5, latp=170, q=64, minp=128, look=0.6):
-    sl = [(int(w[0]), int(w[1])) + {"": (0, K), "a": (0, K // 2), "b": (K // 2, K // 2)}[w[2:]] for w in s.split()]
-    n = len(sl)
-    lo, hi = [x[2] for x in sl], [x[2] + x[3] for x in sl]
-    gend = [[] for _ in sl]
-    need = [[j for j in range(n) if sl[j][:2] == (x[0], x[1] - 1) and (x[1] == 5 or meet(*x[2:], *sl[j][2:]))] for x in sl]
-    made, small, sdone, rank, pdone = {}, {}, {}, {}, set()
-    st, out = {"A": 0.0, "V": 0.0, "P": 0.0}, {"A": [], "V": []}
-
-    def cost(o):
-        return fv + (max(64, sl[o[1]][3] // 4) if o[0] == "S" else 64)
-
-    def lready(i):
-        if sl[i][1] == 5:
-            return made.get(max(need[i]))
-        return max([made[j] for j in need[i]], default=0.0) if all(j in made for j in need[i]) else None
-
-    def give(qn, i, c0, take, t):
-        o = ("G", i, c0, take)
-        out[qn].append(o)
-        st[qn] = rank[o] = t + (fa if qn == "A" else fv) + take * gc
-        gend[i].append((c0, take, st[qn]))
-        for j, (c, k, a0, sn) in enumerate(sl):
-            if k >= 5 or j in pdone:
-                continue
-            if hi[j] > lo[j]:
-                return
-            t, m = st["P"] + sn / 4 * pe, 128 if k % 2 else 32
-            for e in sorted(max(e for a, b, e in gend[j] if meet(a, b, c1, m)) for c1 in range(a0, a0 + sn, m)):
-                t = max(t, e + sync) + (64 if k % 2 else 32) * pe
-            st["P"] = t
-            pdone.add(j)
-            small[("S", j)] = t + latp
-
-    while any(hi[i] > lo[i] for i in range(n)) or small:
-        i = next((i for i in range(n) if hi[i] > lo[i]), None)
-        lr = lready(i) if i is not None else None
-        tA, tV = st["A"], st["V"]
-        if tA <= tV and lr is not None and (max(tA, lr) <= tV or not small):
-            t = max(tA, lr)
-            left = take = hi[i] - lo[i]
-            if left > minp:
-                busy = sum(cost(o) for o, r in small.items() if r < t + left * gc * look)
-                want = (max(tV, lr) + busy - t + left * gc) / (2 * gc)
-                take = max(minp, min(left, int(round(want / q)) * q))
-                if left - take < 64:
-                    take = left
-            hi[i] -= take
-            give("A", i, hi[i], take, t)
-            continue
-        rdy = sorted((r, o) for o, r in small.items())
-        if rdy and (rdy[0][0] <= tV or lr is None or rdy[0][0] <= max(tV, lr) + 30):
-            o = min((o for r, o in rdy if r <= max(tV, rdy[0][0])), key=lambda o: o[1])
-            tV = st["V"] = max(tV, small.pop(o)) + cost(o)
-            out["V"].append(o)
-            c, k = sl[o[1]][:2]
-            if o[0] == "S":
-                sdone[o[1]] = tV
-                js = [j for j in range(n) if sl[j][:2] == (c, 4)]
-                if k < 4:
-                    small[("C", o[1])] = tV + sync
-                elif all(j in sdone for j in js):
-                    small[("T", max(js))] = tV + sync
-            elif o[0] == "T":
-                small[("D", o[1])] = tV + sync
-            else:
-                made[o[1]] = tV + sync
-            continue
-        t = max(tV, lr)
-        take = left = hi[i] - lo[i]
-        if left == sl[i][3]:
-            want = (max(tA, lr) - t + left * gc) / (2 * gc)
-            if rdy:
-                want = min(want, max(64, (rdy[0][0] - t) / gc))
-            take = max(64, min(left, int(round(want / q)) * q))
-        lo[i] += take
-        give("V", i, lo[i] - take, take, t)
-    return sl, out["A"], out["V"], rank
+def rotate():
+    out = {"A": [], "V": [], "P": [("P", i) for i in range(16)], "G": [("C", i) for i in range(12)]}
+    for i, n in enumerate(CFG["share"]):
+        out["V"].append(("G", i, 0, n))
+        out["A"].append(("G", i, n, K - n))
+        if i >= 14:
+            out["V"].append(("D", i - 2))
+        if i >= 1:
+            out["V"].append(("S", i - 1))
+    for q in "AV":
+        for w in CFG["end" + q].split():
+            n = [int(x) for x in w[1:].split(":")]
+            out[q].append(("G", 16 + n[0], n[1], n[2]) if w[0] == "U" else (w[0], *n))
+    return out
 
 
 def peers_of(cores, me, topo):
@@ -131,12 +69,12 @@ def engine_sets(cores, me, topo):
     for n, r in enumerate(far):
         e = topo.engines(c, cores[r])
         part = len(e) // len(far)
-        out[r] = (e[n * part:(n + 1) * part], e, e)
+        out[r] = (e[n * part:(n + 1) * part], e)
         used |= set(e)
     for r in peers_of(cores, me, topo):
         if r not in far:
             e = [x for x in topo.engines(c, cores[r]) if x not in used]
-            out[r] = (e, e, topo.engines(c, cores[r]))
+            out[r] = (e, e)
     return out
 
 
@@ -158,7 +96,7 @@ def rank_program(g, core, T, topo):
 
     Q = {"V": g.vector, "A": g.scalar, "P": g.tensor, "G": g, "Y": g.sync}
     count = {"V": 0, "A": 0, "P": 0, "G": 0}
-    seen, tok = {}, {}
+    seen, tok, left = {}, {}, [0]
 
     def done(q, ins):
         count[q] += 1
@@ -184,31 +122,36 @@ def rank_program(g, core, T, topo):
     V, A, P, Y = g.vector, g.scalar, g.tensor, g.sync
 
     def copy(q, dst, src, add=None):
+        if q == "G":
+            return g.affine_select(dst, src, [[0, dst.shape[1]]], Op.is_ge, 0.0, 0, 0)
         if q == "V":
             return V.tensor_copy(dst, src) if add is None else V.tensor_scalar(dst, src, add, None, Op.add)
         return A.activation(dst, src, Act.Copy) if add is None else A.activation(dst, src, Act.Identity, bias=add)
 
+    def send(items):
+        tr = []
+        for r, e, sem, src, dst in items:
+            rid, pid, _ = topo.addr(cores[r])
+            tr.append(RemoteDMATransfer(dst_ids=[DstId(rid=rid, pnc=pid)], dma_engine_mask=bits(eng[r][e]),
+                                        remote_sem=S[sem % me], src=src, dst=dst))
+            left[0] += len(eng[r][e])
+        g.remote_dma_fused(tr, local_sem=S.left)
+
     pb = [T["pb%d" % b] for b in range(8)]
-    mine = slice(256 * me, 256 * me + 256)
+    w0 = 256 * me
     pieces = CFG["pieces"]
 
     A.dma_start(T.Pl[:], T.place[:]).then_inc(S.lp, 16)
     Y.dma_start(T.Si[:, 0:32], T.when[:]).then_inc(S.lw, 16)
     for h, (c0, n) in enumerate(pieces):
         (Y, A)[h % 2].dma_start(T.tr[0:64, c0:c0 + n], T.track[:, 8 * c0:8 * (c0 + n)]).then_inc(S["lt%d" % h], 16)
-        tok["lt%d" % h] = ("lt%d" % h, 16)
     Y.dma_start(T.U[:], T.sound[:]).then_inc(S.ls, 16)
-    tok.update(lw=("lw", 16), lp=("lp", 16))
+    tok.update({n: (n, 16) for n in ("lw", "lp", "lt0", "lt1", "lt2", "ls")})
 
-    tok["gI"] = done("G", g.iota(T.V[:, 32:160], [[1, 128]], 0, -1))
-    tok["gJ"] = done("G", g.iota(T.V[:, 0:32], [[1, 4], [4, 4], [16, 2]], 0, -1))
-    done("G", g.iota(T.V[:, 160:288], [[1, 8], [8, 16]], 0, -1))
-    tok["gR"] = done("G", g.iota(T.V[:, 288:320], [[1, 2], [34, 4], [8, 4]], 0, -1))
-    tok["pat"] = done("G", g.iota(T.pat[:], [[0, 32], [-32767, 4]], 16384, 0, allow_small_or_imprecise_dtypes=True))
+    def pick(dst, src, pattern, base):
+        return g.affine_select(dst, src, pattern, Op.is_equal, 0.0, base, -1)
 
-    def equal(dst, src, val=0.0, times=None):
-        if times is None:
-            return V.tensor_scalar(dst, src, val, None, Op.is_equal)
+    def equal(dst, src, val=0.0, times=1.0):
         return V.tensor_scalar(dst, src, val, times, Op.is_equal, Op.mult)
 
     def table(q):
@@ -224,9 +167,9 @@ def rank_program(g, core, T, topo):
     def spread(h):
         c0, n = pieces[h]
         for k in range(8):
-            w0, j = 8 * c0 + k * n, 0
+            at, j = 8 * c0 + k * n, 0
             while j < n:
-                b, o = (w0 + j) // 512, (w0 + j) % 512
+                b, o = (at + j) // 512, (at + j) % 512
                 m = min(n - j, 512 - o)
                 if b == 7:
                     wait("P", tok["W"])
@@ -236,10 +179,24 @@ def rank_program(g, core, T, topo):
                     tok["b%d" % b] = done("P", ins)
         return ins
 
+    def add_pairs(q):
+        g.dma_start(T.U[:, 0:L - 1], T.sound[:, 1:L], accum_op=Op.add, max_dma_last_dim=4096).then_inc(S.acc, 16)
+
     start = {
+        "gI": ("", lambda q: g.iota(T.V[:, 32:160], [[1, 128]], 0, -1)),
+        "gJ": ("", lambda q: g.iota(T.V[:, 0:32], [[1, 4], [4, 4], [16, 2]], 0, -1)),
+        "gR0": ("", lambda q: g.iota(T.V[:, 160:288], [[1, 8], [8, 16]], 0, -1)),
+        "gR": ("", lambda q: g.iota(T.V[:, 288:320], [[1, 2], [34, 4], [8, 4]], 0, -1)),
+        "pat": ("", lambda q: g.iota(T.pat[:], [[0, 32], [-32767, 4]], 16384, 0, allow_small_or_imprecise_dtypes=True)),
+        "pm0": ("", lambda q: V.memset(T.pm[:, 0::2], -1.0)),
+        "pm1": ("", lambda q: V.memset(T.pm[:, 1::2], 1.0)),
+        "Ra": ("pm0 pm1", lambda q: pick(T.R[:, 0:256], T.pm[:], [[1, 8], [8, 16], [0, 2]], 0)),
+        "Rb": ("pm0 pm1", lambda q: pick(T.R[:, 256:288], T.pm[:, 0:32], [[34, 4], [8, 4], [0, 2]], 0)),
+        "Rc": ("pm0 pm1", lambda q: pick(T.R[:, 288:320], T.pm[:, 0:32], [[34, 4], [8, 4], [0, 2]], 1)),
         "zIp": ("", lambda q: V.memset(T.Ip[:], 0.0)),
         "zRC": ("", lambda q: V.memset(T.RC[0:96, :], 0.0)),
-        "zW": ("", lambda q: V.memset(T.W[96:128, mine], 0.0)),
+        "zW": ("", lambda q: V.memset(T.W[96:128, w0:w0 + 256], 1.0)),
+        "cRC": ("", lambda q: V.memset(T.RC[96:128, :], HALF / 32)),
         "I": ("gI", lambda q: equal(T.Irep[:, 0:128], T.V[:, 32:160])),
         "Ip": ("I zIp", lambda q: copy(q, T.Ip[:, 128:256], T.Irep[:, 0:128])),
         "I2": ("I", lambda q: copy(q, T.Irep[:, 128:256], T.Irep[:, 0:128])),
@@ -247,15 +204,18 @@ def rank_program(g, core, T, topo):
         "I8": ("I4", lambda q: copy(q, T.Irep[:, 512:1024], T.Irep[:, 0:512])),
         "J": ("gJ", lambda q: equal(T.J[0:32, :], T.V[0:32, 0:64])),
         "R": ("gR", lambda q: equal(T.R[:, 1::2], T.V[:, 160:320])),
-        "nR": ("R", lambda q: A.activation(T.R[:, 0::2], T.R[:, 1::2], Act.Identity, scale=-1.0) if q == "A"
-               else equal(T.R[:, 0::2], T.V[:, 160:320], 0.0, -1.0)),
+        "nR": ("R", lambda q: A.activation(T.R[:, 0::2], T.R[:, 1::2], Act.Identity, scale=-1.0)),
         "x": ("lp", lambda q: V.tensor_scalar(T.Si[:, 32:64], T.Pl[:], 12, None, Op.logical_shift_right)),
         "y": ("lp", lambda q: V.tensor_scalar(T.Si[:, 64:96], T.Pl[:], 4095, None, Op.bitwise_and)),
         "ht": ("lw", lambda q: copy(q, T.Sh[:, 0:32], T.Si[:, 0:32], -HALF)),
         "hxy": ("x y", lambda q: copy(q, T.Sh[:, 32:96], T.Si[:, 32:96], -HALF)),
         "T": ("lw", lambda q: V.transpose(T.tz[:], T.Si[:, 0:32])),
         "off": ("T", lambda q: copy(q, T.off[:, 96:128], T.tz[:])),
-        "W": ("W0 W1 W2", lambda q: copy(q, T.W[0:96, mine], pb[7][0:96, 0:256])),
+        "W": ("W0 W1 W2", lambda q: copy(q, T.W[0:96, w0:w0 + 256], pb[7][0:96, 0:256])),
+        "sendO": ("off", lambda q: send([(r, 0, "qo%d", T.off[:, 96:128], T.off[:, 32 * back[r]:32 * back[r] + 32]) for r in peers])),
+        "sendA": ("zW W", lambda q: send([(r, 0, "qa%d", T.W[:, w0:w0 + 128], T.W[:, w0:w0 + 128]) for r in peers])),
+        "sendZ": ("zW W", lambda q: send([(r, 0, "qz%d", T.W[:, w0 + 128:w0 + 256], T.W[:, w0 + 128:w0 + 256]) for r in peers])),
+        "add": ("ls", add_pairs),
     }
     for n in range(4):
         p = 32 + 32 * (n // 2)
@@ -276,107 +236,64 @@ def rank_program(g, core, T, topo):
 
     def begin(q, name):
         wait(q, *[tok[d] for d in start[name][0].split()])
-        return done(q, start[name][1](q))
+        ins = start[name][1](q)
+        return None if ins is None else done(q, ins)
 
-    run({q: CFG[q].split() for q in "VAP"},
+    run({q: CFG[q].split() for q in "GVAP"},
         lambda name: start[name][0].split() + (["W"] if name == "p%d" % (len(pieces) - 1) else []), begin)
     window = [tok["e%d" % b] for b in range(8)]
-    consts = [tok[n] for n in ("R", "nR", "RC0", "RC1", "RC2", "RC3", "t0", "t1", "t2", "t3")]
+    consts = [tok[n] for n in ("zW", "cRC", "R", "nR", "RC0", "RC1", "RC2", "RC3", "t0", "t1", "t2", "t3", "Ra", "Rb", "Rc") if n in tok]
 
-    left = [0]
-
-    def send(items):
-        tr = []
-        for r, e, sem, src, dst in items:
-            rid, pid, _ = topo.addr(cores[r])
-            tr.append(RemoteDMATransfer(dst_ids=[DstId(rid=rid, pnc=pid)], dma_engine_mask=bits(eng[r][e]),
-                                        remote_sem=S[sem % me], src=src, dst=dst))
-            left[0] += len(eng[r][e])
-        g.remote_dma_fused(tr, local_sem=S.left)
-
-    wait("G", tok["off"])
-    send([(r, 0, "qo%d", T.off[:, 96:128], T.off[:, 32 * back[r]:32 * back[r] + 32]) for r in peers])
-    wait("G", tok["zW"], tok["W"])
-    for n in range(CFG["wcalls"]):
-        w = 256 // CFG["wcalls"]
-        ap = T.W[:, 256 * me + w * n:256 * me + w * n + w]
-        send([(r, 0, ("qw%d", "qz%d")[n], ap, ap) for r in peers])
-    wait("G", ("ls", 16))
-    g.dma_start(T.U[:, 0:L - 1], T.sound[:, 1:L], accum_op=Op.add, max_dma_last_dim=4096).then_inc(S.acc, 16)
-
-    slots, order_A, order_V, rank = CFG["plan"] if "plan" in CFG else deal(CFG["slots"], CFG["gc"], **CFG["deal"])
-    place = {}
-    for c, k, _, _ in slots:
-        if k < 5 and (c, k) not in place:
-            place[(c, k)] = len(place)
-    lst = {(c, 1): 32 * c for c in range(N)}
-    lst.update({(c, k + 1): 128 + 32 * place[(c, k)] for c, k in place})
-    last_read = {}
-    allG = [o for o in order_A + order_V if o[0] == "G"]
-    order_P = [("P", i) for i, sl in enumerate(slots) if sl[1] < 5]
+    order = rotate()
+    gathers = {i: [o for q in ("AV" if i < CFG["flip"] else "VA") for o in order[q] if o[:2] == ("G", i)] for i in range(20)}
 
     def ready(op):
         kind, i = op[:2]
-        c, k = slots[i][:2]
         if kind == "G":
-            if k == 5:
-                return [("D", max(j for j, sl in enumerate(slots) if sl[:2] == (c, 4)))]
-            return [("C", j) for j, sl in enumerate(slots) if sl[:2] == (c, k - 1) and meet(*op[2:], *sl[2:])]
-        if kind == "P":
-            return [o for o in allG if o[1] == i]
-        if kind == "T":
-            return [("S", j) for j, sl in enumerate(slots) if sl[:2] == (c, 4)]
-        return [({"S": "P", "C": "S", "D": "T"}[kind], i)]
+            return [] if i < 4 else [("C" if i < 16 else "D", i - 4)]
+        return gathers[i] if kind == "P" else [("P" if kind == "S" else "S", i)]
 
     def emit(q, op):
         kind, i = op[:2]
         deps = [tok[d] for d in ready(op)]
-        c, k, first, cols = slots[i]
-        r, ps = chunk_rank[c], pb[i % 4]
+        c, k = i % N, i // N + 1
+        r, ps = chunk_rank[c], pb[c]
         if kind == "G":
             c0, n = op[2:]
             if k == 1:
                 wait(q, *window, tok["off"] if r == me else ("qo%d" % r, len(came[r][0])))
             wait(q, *deps)
-            offs = T.off[:, lst[(c, k)] + c0 // 16:lst[(c, k)] + (c0 + n) // 16]
+            offs = T.off[:, 32 * i + c0 // 16:32 * i + (c0 + n) // 16]
             if k == 5:
                 wait(q, ("acc", 16))
                 return done(q, copy(q, (T.ui if r == me else T.uo)[:, K * c + c0:K * c + c0 + n], T.U[:, :].indirect(offs)))
-            return done(q, copy(q, T.gb[:, K * place[(c, k)] + c0:K * place[(c, k)] + c0 + n], T.win[:, :].indirect(offs)))
+            return done(q, copy(q, T.gb[:, K * i + c0:K * i + c0 + n], T.win[:, :].indirect(offs)))
         if kind == "P":
-            wait(q, *window, *consts, *last_read.get(i % 4, []))
-            lay, g0, a, b = (0 if k % 2 else 128), K * place[(c, k)], first // 4, (first + cols) // 4
-            wait(q, tok["W"] if r == me else (("qw%d" if k == 1 or CFG["wcalls"] == 1 else "qz%d") % r, len(came[r][0])))
-            P.matmul(ps[:, a:b], T.W[0:96, 256 * r + lay:256 * r + lay + 128], T.RC[0:96, lay + a:lay + b], True, False)
-            ss = range(first // 128, (first + cols) // 128)
+            wait(q, *window, *consts, *([tok[("S", i - N)]] if k > 1 else []))
+            lay = 0 if k % 2 else 128
+            wait(q, tok["W"] if r == me else (("qa%d" if k == 1 else "qz%d") % r, len(came[r][0])))
+            P.matmul(ps[:, 0:128], T.W[:, 256 * r + lay:256 * r + lay + 128], T.RC[:, lay:lay + 128], True, False)
             if k % 2:
-                sets = [(128 * s, 128, ps[:, 32 * s:32 * s + 32], 256 + 32 * (s // 2)) for s in ss]
+                sets = [(128 * s, 128, ps[:, 32 * s:32 * s + 32], 256 + 32 * (s // 2)) for s in range(4)]
             else:
                 sets = [(128 * s + 32 * z, 32, ps[32 * z:32 * z + 32, 32 * s:32 * s + 32], 32 * (2 * z + s // 2))
-                        for s in ss for z in range(4)]
-            gs = sorted(ready(op), key=lambda o: rank[o])
-            sets.sort(key=lambda st: max(n for n, o in enumerate(gs) if meet(*o[2:], *st[:2])))
+                        for s in range(4) for z in range(4)]
+            sets.sort(key=lambda st: max(n for n, o in enumerate(gathers[i]) if meet(*o[2:], *st[:2])))
             for n, (c0, m, out, rc) in enumerate(sets):
-                wait(q, *[tok[o] for o in gs if meet(*o[2:], c0, m)])
-                ins = P.matmul(out, T.gb[:, g0 + c0:g0 + c0 + m], T.R[:, rc:rc + 32], False,
+                wait(q, *[tok[o] for o in gathers[i] if meet(*o[2:], c0, m)])
+                ins = P.matmul(out, T.gb[:, K * i + c0:K * i + c0 + m], T.R[:, rc:rc + 32], False,
                                all(st[0] % 128 != c0 % 128 for st in sets[n + 1:]))
             return done(q, ins)
         wait(q, tok["pat"], *deps)
-        p0 = place[(c, k)]
-        a, b = (0, 128) if kind in "TD" else (first // 4, (first + cols) // 4)
-        sc3, tt = T.sc[:, 128 * p0 + a + 3:128 * p0 + b:4], T.tt[:, 32 * p0:32 * p0 + 32]
         if kind == "S":
-            ins = V.tensor_tensor_scan(T.sc[:, 128 * p0 + a:128 * p0 + b], T.pat[:, 0:b - a], ps[:, a:b], 0.0, Op.max, Op.min)
-            last_read[i % 4] = [done(q, ins)]
-            return last_read[i % 4][0]
-        if kind == "T":
-            return done(q, V.transpose(tt, sc3))
-        return done(q, copy(q, T.off[:, 128 + 32 * p0 + a // 4:128 + 32 * p0 + b // 4], sc3 if kind == "C" else tt, HALF))
+            return done(q, V.tensor_tensor_scan(T.sc[:, 128 * i:128 * i + 128], T.pat[:], ps[:, 0:128], 0.0, Op.max, Op.min))
+        dst, src = T.off[:, 32 * (i + N):32 * (i + N) + 32], T.sc[:, 128 * i + 3:128 * i + 128:4]
+        return done(q, V.transpose(dst, src) if kind == "D" else copy(q, dst, src))
 
-    run({"A": list(order_A), "V": list(order_V), "P": order_P}, ready, emit)
+    run(order, ready, emit)
 
     def sound_of(c, c0, m):
-        return [tok[o] for o in allG if slots[o[1]][:2] == (c, 5) and meet(*o[2:], c0, m)]
+        return [tok[o] for o in gathers[16 + c] if meet(*o[2:], c0, m)]
 
     for cs in CFG["sends"]:
         for c, e, c0, m in cs:
@@ -391,22 +308,31 @@ def rank_program(g, core, T, topo):
     while pre < N - 1 and chunk_rank.index(seq[pre]) in CFG["pre"]:
         pre += 1
     H, summed = range(len(fin)), {}
-    for n, h in [(n, h) for n in range(pre) for h in H] + [(n, h) for h in H for n in range(pre, N)]:
-        r, (c0, m, _) = seq[n], fin[h]
+
+    def term(q, r, c0, m):
         c = chunk_rank.index(r)
         if r == me:
-            wait("P", *sound_of(c, c0, m))
+            wait(q, *sound_of(c, c0, m))
         else:
-            wait("P", *[(("qv%d" if a else "qu%d") % r, len(came[r][e])) for cc, e, a, w in sent if cc == back[r] and meet(a, w, c0, m)])
-        ins = P.matmul(pb[4 + h][:, 0:m], T.Irep[:, 0:128], T.ui[:, K * c + c0:K * c + c0 + m], n == 0, n == N - 1)
-        if n == N - 1:
+            wait(q, *[(("qv%d" if a else "qu%d") % r, len(came[r][e])) for cc, e, a, w in sent if cc == back[r] and meet(a, w, c0, m)])
+        return T.ui[:, K * c + c0:K * c + c0 + m]
+
+    for n, h in [(n, h) for n in range(pre) for h in H] + [(n, h) for h in H for n in range(pre, N)]:
+        c0, m, q = fin[h]
+        last = N - 2 if q == "V" and CFG["fuse"] else N - 1
+        if n <= last:
+            ins = P.matmul(pb[4 + h][:, 0:m], T.Irep[:, 0:128], term("P", seq[n], c0, m), n == 0, n == last)
+        if n == last:
             summed[h] = done("P", ins)
     for h, (c0, m, q) in enumerate(fin):
         wait(q, summed[h])
-        a = done(q, copy(q, T.ysb[:, c0:c0 + m], pb[4 + h][:, 0:m]))
-        sq = "A" if h == len(fin) - 1 else "Y"
+        if q == "V" and CFG["fuse"]:
+            a = done(q, V.tensor_tensor(T.ysb[:, c0:c0 + m], pb[4 + h][:, 0:m], term(q, seq[N - 1], c0, m), Op.add))
+        else:
+            a = done(q, copy(q, T.ysb[:, c0:c0 + m], pb[4 + h][:, 0:m]))
+        sq = CFG["stq"][h]
         wait(sq, a)
         Q[sq].dma_start(T.y[:, c0:c0 + m], T.ysb[:, c0:c0 + m]).then_inc(S.st, 16)
 
-    wait("G", ("left", left[0]), ("sV", count["V"]), ("sA", count["A"]), ("sP", count["P"]), ("sG", count["G"]),
-         ("st", 16 * len(fin)))
+    wait("G", ("left", left[0]), ("sG", count["G"]))
+    wait("V", ("sV", count["V"]), ("sA", count["A"]), ("sP", count["P"]), ("st", 16 * len(fin)))

from concourse.bass import DstId, RemoteDMATransfer
from concourse.mybir import AluOpType as Op, ActivationFunctionType as Act

N, L, K = 4, 4096, 512
HALF = 2048.0

SCRATCH = {
    "Si": ("sbuf", [128, 96], "int32"), "Pl": ("sbuf", [128, 32], "int32"), "tz": ("sbuf", [128, 32], "int32"),
    "Sh": ("sbuf", [128, 96], "float16"), "Ip": ("sbuf", [128, 384], "float16"),
    "off": ("sbuf", [128, 32 * 20], "uint16"), "W": ("sbuf", [128, N * 256], "float16"),
    "tr": ("sbuf", [128, 512], "int32"), "xi": ("sbuf", [128, 512], "int32"), "xh": ("sbuf", [128, 512], "float16"),
    "win": ("sbuf", [128, L], "float32"), "U": ("sbuf", [128, L], "bfloat16"),
    "gb": ("sbuf", [128, K * 16], "float16"), "sc": ("sbuf", [128, 128 * 16], "uint16"),
    "uo": ("sbuf", [128, N * K], "bfloat16"), "ui": ("sbuf", [128, N * K], "bfloat16"),
    "ysb": ("sbuf", [128, K], "float32"),
    "V": ("sbuf", [128, 320], "int32"), "J": ("sbuf", [128, 64], "float16"),
    "Irep": ("sbuf", [128, 1024], "bfloat16"),
    "R": ("sbuf", [128, 320], "float16"), "RC": ("sbuf", [128, 256], "float16"),
    "pat": ("sbuf", [128, 128], "float32"), "pm": ("sbuf", [128, 256], "float16"),
}
for _b in range(8):
    SCRATCH["pb%d" % _b] = ("psum", [128, 512], "float32")

SEMAPHORES = (["sV", "sA", "sP", "sG", "lw", "lp", "lt0", "lt1", "lt2", "ls", "acc", "left", "st"]
              + ["%s%d" % (n, q) for n in ("qo", "qa", "qz", "qu", "qv") for q in range(N)])

CFG = {"pieces": [(0, 128), (128, 128), (256, 256)],
       "V": "pm0 zIp pm1 zRC I J I2 T x y off X0 Y0 X1 Y1 X2 Y2 h1 zW e0 e2 e4 e6 RC0 RC1 RC2 RC3 cRC",
       "A": "Ip ht I4 hxy I8 h0 t0 W h2 e1 e3 e5 e7 t1 t2",
       "P": "W0 W1 W2 p0 p1 p2",
       "G": "gI gJ Ra sendO sendA sendZ Rb Rc t3 pat add",
       "share": [256, 256] + [192, 192, 224] * 4 + [192, 192], "flip": 12, "stq": "YYYA", "fuse": True,
       "endV": "U0:384:128 D14 S15 U2:0:256 D15 U2:256:160 U3:0:256",
       "endA": "U0:0:192 U0:192:192 U1:0:256 U1:256:256 U2:416:96 U3:256:256",
       "sends": [[(0, 1, 0, 192)], [(0, 1, 192, 320)], [(1, 1, 0, 256), (2, 1, 0, 256)], [(1, 1, 256, 256), (2, 1, 256, 256)]],
       "late": [0, 3, 1, 2], "pre": [0, 3], "fin": [(0, 128, "V"), (128, 128, "A"), (256, 128, "V"), (384, 128, "A")]}


def meet(a, n, b, m):
    return a < b + m and b < a + n


def rotate():
    out = {"A": [], "V": [], "P": [("P", i) for i in range(16)], "G": [("C", i) for i in range(12)]}
    for i, n in enumerate(CFG["share"]):
        out["V"].append(("G", i, 0, n))
        out["A"].append(("G", i, n, K - n))
        if i >= 14:
            out["V"].append(("D", i - 2))
        if i >= 1:
            out["V"].append(("S", i - 1))
    for q in "AV":
        for w in CFG["end" + q].split():
            n = [int(x) for x in w[1:].split(":")]
            out[q].append(("G", 16 + n[0], n[1], n[2]) if w[0] == "U" else (w[0], *n))
    return out


def peers_of(cores, me, topo):
    c = cores[me]
    others = [r for r in range(len(cores)) if r != me]
    return sorted(others, key=lambda r: (topo.chip(cores[r]) == topo.chip(c), topo.die(cores[r]) == topo.die(c), r))


def engine_sets(cores, me, topo):
    c = cores[me]
    far = [r for r in peers_of(cores, me, topo) if topo.chip(cores[r]) != topo.chip(c)]
    out, used = {}, set()
    for n, r in enumerate(far):
        e = topo.engines(c, cores[r])
        part = len(e) // len(far)
        out[r] = (e[n * part:(n + 1) * part], e)
        used |= set(e)
    for r in peers_of(cores, me, topo):
        if r not in far:
            e = [x for x in topo.engines(c, cores[r]) if x not in used]
            out[r] = (e, e)
    return out


def bits(e):
    return sum(1 << x for x in e)


def rank_program(g, core, T, topo):
    me = T.rank_of(core)
    if me is None:
        return
    cores = list(T.cores)
    S = T.sem
    peers = peers_of(cores, me, topo)
    chunk_rank = peers + [me]
    eng = engine_sets(cores, me, topo)
    came = {q: engine_sets(cores, q, topo)[me] for q in peers}
    back = {r: peers_of(cores, r, topo).index(me) for r in peers}

    Q = {"V": g.vector, "A": g.scalar, "P": g.tensor, "G": g, "Y": g.sync}
    count = {"V": 0, "A": 0, "P": 0, "G": 0}
    seen, tok, left = {}, {}, [0]

    def done(q, ins):
        count[q] += 1
        ins.then_inc(S["s" + q], 1)
        return ("s" + q, count[q])

    def wait(q, *toks):
        for name, val in toks:
            if seen.get((q, name), 0) < val:
                Q[q].wait_ge(S[name], val)
                seen[(q, name)] = val

    def run(todo, ready, emit):
        while any(todo.values()):
            moved = False
            for q in todo:
                while todo[q] and all(d in tok for d in ready(todo[q][0])):
                    op = todo[q].pop(0)
                    tok[op] = emit(q, op)
                    moved = True
            assert moved, todo

    V, A, P, Y = g.vector, g.scalar, g.tensor, g.sync

    def copy(q, dst, src, add=None):
        if q == "G":
            return g.affine_select(dst, src, [[0, dst.shape[1]]], Op.is_ge, 0.0, 0, 0)
        if q == "V":
            return V.tensor_copy(dst, src) if add is None else V.tensor_scalar(dst, src, add, None, Op.add)
        return A.activation(dst, src, Act.Copy) if add is None else A.activation(dst, src, Act.Identity, bias=add)

    def send(items):
        tr = []
        for r, e, sem, src, dst in items:
            rid, pid, _ = topo.addr(cores[r])
            tr.append(RemoteDMATransfer(dst_ids=[DstId(rid=rid, pnc=pid)], dma_engine_mask=bits(eng[r][e]),
                                        remote_sem=S[sem % me], src=src, dst=dst))
            left[0] += len(eng[r][e])
        g.remote_dma_fused(tr, local_sem=S.left)

    pb = [T["pb%d" % b] for b in range(8)]
    w0 = 256 * me
    pieces = CFG["pieces"]

    A.dma_start(T.Pl[:], T.place[:]).then_inc(S.lp, 16)
    Y.dma_start(T.Si[:, 0:32], T.when[:]).then_inc(S.lw, 16)
    for h, (c0, n) in enumerate(pieces):
        (Y, A)[h % 2].dma_start(T.tr[0:64, c0:c0 + n], T.track[:, 8 * c0:8 * (c0 + n)]).then_inc(S["lt%d" % h], 16)
    Y.dma_start(T.U[:], T.sound[:]).then_inc(S.ls, 16)
    tok.update({n: (n, 16) for n in ("lw", "lp", "lt0", "lt1", "lt2", "ls")})

    def pick(dst, src, pattern, base):
        return g.affine_select(dst, src, pattern, Op.is_equal, 0.0, base, -1)

    def equal(dst, src, val=0.0, times=1.0):
        return V.tensor_scalar(dst, src, val, times, Op.is_equal, Op.mult)

    def table(q):
        rows = slice(32 * q, 32 * q + 32)
        for il in range(8):
            o = pb[7][rows, 16 * il:16 * il + 16]
            P.matmul(o, T.Ip[:, 128 + il:384:8], T.Sh[:, 32 * q:32 * q + 16], True, False)
            P.matmul(o, T.Ip[:, il:256:8], T.Sh[:, 32 * q + 16:32 * q + 32], False, True)
        for z in range(4):
            ins = P.matmul(pb[7][rows, 128 + 32 * z:160 + 32 * z], T.Ip[:, 128 + 32 * z:160 + 32 * z], T.Sh[:, rows], True, True)
        return ins

    def spread(h):
        c0, n = pieces[h]
        for k in range(8):
            at, j = 8 * c0 + k * n, 0
            while j < n:
                b, o = (at + j) // 512, (at + j) % 512
                m = min(n - j, 512 - o)
                if b == 7:
                    wait("P", tok["W"])
                ins = P.matmul(pb[b][:, o:o + m], T.Irep[:, k::8], T.xh[:, c0 + j:c0 + j + m], True, True)
                j += m
                if o + m == 512 and (k < 7 or j < n):
                    tok["b%d" % b] = done("P", ins)
        return ins

    def add_pairs(q):
        g.dma_start(T.U[:, 0:L - 1], T.sound[:, 1:L], accum_op=Op.add, max_dma_last_dim=4096).then_inc(S.acc, 16)

    start = {
        "gI": ("", lambda q: g.iota(T.V[:, 32:160], [[1, 128]], 0, -1)),
        "gJ": ("", lambda q: g.iota(T.V[:, 0:32], [[1, 4], [4, 4], [16, 2]], 0, -1)),
        "gR0": ("", lambda q: g.iota(T.V[:, 160:288], [[1, 8], [8, 16]], 0, -1)),
        "gR": ("", lambda q: g.iota(T.V[:, 288:320], [[1, 2], [34, 4], [8, 4]], 0, -1)),
        "pat": ("", lambda q: g.iota(T.pat[:], [[0, 32], [-32767, 4]], 16384, 0, allow_small_or_imprecise_dtypes=True)),
        "pm0": ("", lambda q: V.memset(T.pm[:, 0::2], -1.0)),
        "pm1": ("", lambda q: V.memset(T.pm[:, 1::2], 1.0)),
        "Ra": ("pm0 pm1", lambda q: pick(T.R[:, 0:256], T.pm[:], [[1, 8], [8, 16], [0, 2]], 0)),
        "Rb": ("pm0 pm1", lambda q: pick(T.R[:, 256:288], T.pm[:, 0:32], [[34, 4], [8, 4], [0, 2]], 0)),
        "Rc": ("pm0 pm1", lambda q: pick(T.R[:, 288:320], T.pm[:, 0:32], [[34, 4], [8, 4], [0, 2]], 1)),
        "zIp": ("", lambda q: V.memset(T.Ip[:], 0.0)),
        "zRC": ("", lambda q: V.memset(T.RC[0:96, :], 0.0)),
        "zW": ("", lambda q: V.memset(T.W[96:128, w0:w0 + 256], 1.0)),
        "cRC": ("", lambda q: V.memset(T.RC[96:128, :], HALF / 32)),
        "I": ("gI", lambda q: equal(T.Irep[:, 0:128], T.V[:, 32:160])),
        "Ip": ("I zIp", lambda q: copy(q, T.Ip[:, 128:256], T.Irep[:, 0:128])),
        "I2": ("I", lambda q: copy(q, T.Irep[:, 128:256], T.Irep[:, 0:128])),
        "I4": ("I2", lambda q: copy(q, T.Irep[:, 256:512], T.Irep[:, 0:256])),
        "I8": ("I4", lambda q: copy(q, T.Irep[:, 512:1024], T.Irep[:, 0:512])),
        "J": ("gJ", lambda q: equal(T.J[0:32, :], T.V[0:32, 0:64])),
        "R": ("gR", lambda q: equal(T.R[:, 1::2], T.V[:, 160:320])),
        "nR": ("R", lambda q: A.activation(T.R[:, 0::2], T.R[:, 1::2], Act.Identity, scale=-1.0)),
        "x": ("lp", lambda q: V.tensor_scalar(T.Si[:, 32:64], T.Pl[:], 12, None, Op.logical_shift_right)),
        "y": ("lp", lambda q: V.tensor_scalar(T.Si[:, 64:96], T.Pl[:], 4095, None, Op.bitwise_and)),
        "ht": ("lw", lambda q: copy(q, T.Sh[:, 0:32], T.Si[:, 0:32], -HALF)),
        "hxy": ("x y", lambda q: copy(q, T.Sh[:, 32:96], T.Si[:, 32:96], -HALF)),
        "T": ("lw", lambda q: V.transpose(T.tz[:], T.Si[:, 0:32])),
        "off": ("T", lambda q: copy(q, T.off[:, 96:128], T.tz[:])),
        "W": ("W0 W1 W2", lambda q: copy(q, T.W[0:96, w0:w0 + 256], pb[7][0:96, 0:256])),
        "sendO": ("off", lambda q: send([(r, 0, "qo%d", T.off[:, 96:128], T.off[:, 32 * back[r]:32 * back[r] + 32]) for r in peers])),
        "sendA": ("zW W", lambda q: send([(r, 0, "qa%d", T.W[:, w0:w0 + 128], T.W[:, w0:w0 + 128]) for r in peers])),
        "sendZ": ("zW W", lambda q: send([(r, 0, "qz%d", T.W[:, w0 + 128:w0 + 256], T.W[:, w0 + 128:w0 + 256]) for r in peers])),
        "add": ("ls", add_pairs),
    }
    for n in range(4):
        p = 32 + 32 * (n // 2)
        start["RC%d" % n] = ("gJ zRC", lambda q, n=n, p=p: equal(T.RC[p:p + 32, n::4], T.V[p:p + 32, 0:64], -float(p), 1.0 - 2.0 * (n % 2)))
        start["t%d" % n] = ("J zRC", lambda q, n=n: copy(q, T.RC[0:32, n::4], T.J[0:32, :]))
    for n in range(3):
        start["W%d" % n] = ("Ip hxy" if n else "Ip ht", lambda q, n=n: table(n))
    for h, (c0, n) in enumerate(pieces):
        c = slice(c0, c0 + n)
        start["X%d" % h] = ("lt%d" % h, lambda q, c=c: V.tensor_scalar(T.xi[0:64, c], T.tr[0:64, c], 12, None, Op.logical_shift_right))
        start["Y%d" % h] = ("lt%d" % h, lambda q, c=c: V.tensor_scalar(T.xi[64:128, c], T.tr[0:64, c], 4095, None, Op.bitwise_and))
        start["h%d" % h] = ("X%d Y%d" % (h, h), lambda q, c=c: copy(q, T.xh[:, c], T.xi[:, c], -HALF))
        last = 8 * (c0 + n) // 512 - 1
        start["p%d" % h] = ("I8 h%d" % h, lambda q, h=h: spread(h))
        for b in range(8 * c0 // 512, last + 1):
            start["e%d" % b] = ("b%d" % b if b < last else "p%d" % h,
                                lambda q, b=b: copy(q, T.win[:, 512 * b:512 * b + 512], pb[b][:]))

    def begin(q, name):
        wait(q, *[tok[d] for d in start[name][0].split()])
        ins = start[name][1](q)
        return None if ins is None else done(q, ins)

    run({q: CFG[q].split() for q in "GVAP"},
        lambda name: start[name][0].split() + (["W"] if name == "p%d" % (len(pieces) - 1) else []), begin)
    window = [tok["e%d" % b] for b in range(8)]
    consts = [tok[n] for n in ("zW", "cRC", "R", "nR", "RC0", "RC1", "RC2", "RC3", "t0", "t1", "t2", "t3", "Ra", "Rb", "Rc") if n in tok]

    order = rotate()
    gathers = {i: [o for q in ("AV" if i < CFG["flip"] else "VA") for o in order[q] if o[:2] == ("G", i)] for i in range(20)}

    def ready(op):
        kind, i = op[:2]
        if kind == "G":
            return [] if i < 4 else [("C" if i < 16 else "D", i - 4)]
        return gathers[i] if kind == "P" else [("P" if kind == "S" else "S", i)]

    def emit(q, op):
        kind, i = op[:2]
        deps = [tok[d] for d in ready(op)]
        c, k = i % N, i // N + 1
        r, ps = chunk_rank[c], pb[c]
        if kind == "G":
            c0, n = op[2:]
            if k == 1:
                wait(q, *window, tok["off"] if r == me else ("qo%d" % r, len(came[r][0])))
            wait(q, *deps)
            offs = T.off[:, 32 * i + c0 // 16:32 * i + (c0 + n) // 16]
            if k == 5:
                wait(q, ("acc", 16))
                return done(q, copy(q, (T.ui if r == me else T.uo)[:, K * c + c0:K * c + c0 + n], T.U[:, :].indirect(offs)))
            return done(q, copy(q, T.gb[:, K * i + c0:K * i + c0 + n], T.win[:, :].indirect(offs)))
        if kind == "P":
            wait(q, *window, *consts, *([tok[("S", i - N)]] if k > 1 else []))
            lay = 0 if k % 2 else 128
            wait(q, tok["W"] if r == me else (("qa%d" if k == 1 else "qz%d") % r, len(came[r][0])))
            P.matmul(ps[:, 0:128], T.W[:, 256 * r + lay:256 * r + lay + 128], T.RC[:, lay:lay + 128], True, False)
            if k % 2:
                sets = [(128 * s, 128, ps[:, 32 * s:32 * s + 32], 256 + 32 * (s // 2)) for s in range(4)]
            else:
                sets = [(128 * s + 32 * z, 32, ps[32 * z:32 * z + 32, 32 * s:32 * s + 32], 32 * (2 * z + s // 2))
                        for s in range(4) for z in range(4)]
            sets.sort(key=lambda st: max(n for n, o in enumerate(gathers[i]) if meet(*o[2:], *st[:2])))
            for n, (c0, m, out, rc) in enumerate(sets):
                wait(q, *[tok[o] for o in gathers[i] if meet(*o[2:], c0, m)])
                ins = P.matmul(out, T.gb[:, K * i + c0:K * i + c0 + m], T.R[:, rc:rc + 32], False,
                               all(st[0] % 128 != c0 % 128 for st in sets[n + 1:]))
            return done(q, ins)
        wait(q, tok["pat"], *deps)
        if kind == "S":
            return done(q, V.tensor_tensor_scan(T.sc[:, 128 * i:128 * i + 128], T.pat[:], ps[:, 0:128], 0.0, Op.max, Op.min))
        dst, src = T.off[:, 32 * (i + N):32 * (i + N) + 32], T.sc[:, 128 * i + 3:128 * i + 128:4]
        return done(q, V.transpose(dst, src) if kind == "D" else copy(q, dst, src))

    run(order, ready, emit)

    def sound_of(c, c0, m):
        return [tok[o] for o in gathers[16 + c] if meet(*o[2:], c0, m)]

    for cs in CFG["sends"]:
        for c, e, c0, m in cs:
            wait("G", *sound_of(c, c0, m))
        send([(chunk_rank[c], e, "qv%d" if c0 else "qu%d", T.uo[:, K * c + c0:K * c + c0 + m],
               T.ui[:, K * back[chunk_rank[c]] + c0:K * back[chunk_rank[c]] + c0 + m]) for c, e, c0, m in cs])
    sent = [x for cs in CFG["sends"] for x in cs]

    fin, late = CFG["fin"], CFG["late"]
    seq = [1, 0, 2, 3] if late.index(chunk_rank.index(0)) > late.index(chunk_rank.index(1)) else [0, 1, 2, 3]
    pre = 0
    while pre < N - 1 and chunk_rank.index(seq[pre]) in CFG["pre"]:
        pre += 1
    H, summed = range(len(fin)), {}

    def term(q, r, c0, m):
        c = chunk_rank.index(r)
        if r == me:
            wait(q, *sound_of(c, c0, m))
        else:
            wait(q, *[(("qv%d" if a else "qu%d") % r, len(came[r][e])) for cc, e, a, w in sent if cc == back[r] and meet(a, w, c0, m)])
        return T.ui[:, K * c + c0:K * c + c0 + m]

    for n, h in [(n, h) for n in range(pre) for h in H] + [(n, h) for h in H for n in range(pre, N)]:
        c0, m, q = fin[h]
        last = N - 2 if q == "V" and CFG["fuse"] else N - 1
        if n <= last:
            ins = P.matmul(pb[4 + h][:, 0:m], T.Irep[:, 0:128], term("P", seq[n], c0, m), n == 0, n == last)
        if n == last:
            summed[h] = done("P", ins)
    for h, (c0, m, q) in enumerate(fin):
        wait(q, summed[h])
        if q == "V" and CFG["fuse"]:
            a = done(q, V.tensor_tensor(T.ysb[:, c0:c0 + m], pb[4 + h][:, 0:m], term(q, seq[N - 1], c0, m), Op.add))
        else:
            a = done(q, copy(q, T.ysb[:, c0:c0 + m], pb[4 + h][:, 0:m]))
        sq = CFG["stq"][h]
        wait(sq, a)
        Q[sq].dma_start(T.y[:, c0:c0 + m], T.ysb[:, c0:c0 + m]).then_inc(S.st, 16)

    wait("G", ("left", left[0]), ("sG", count["G"]))
    wait("V", ("sV", count["V"]), ("sA", count["A"]), ("sP", count["P"]), ("st", 16 * len(fin)))
